import numpy as np
import ml_dtypes


def mxq(x, axis, fmt="e4m3"):
    dtype, down = {"e4m3": (ml_dtypes.float8_e4m3fn, 7), "e5m2": (ml_dtypes.float8_e5m2, 14)}[fmt]
    v = np.moveaxis(np.asarray(x, np.float32).astype(ml_dtypes.bfloat16).astype(np.float64), axis, -1)
    blocks = v.reshape(v.shape[:-1] + (-1, 32))
    amax = np.abs(blocks).max(-1, keepdims=True)
    byte = np.maximum(np.where(amax > 0, np.frexp(amax)[1] - 1 + 127, 0) - down, 1)
    scale = np.exp2(byte - 127.0)
    codes = (blocks / scale).astype(np.float32).astype(dtype).astype(np.float64)
    return np.moveaxis((codes * scale).reshape(v.shape), -1, axis)


WIDE = False


def mx_kscale(k):
    if not WIDE:
        return np.ones(k)
    levels = np.array([10, -10, 5, -5, 0])
    if k % 512:
        return np.exp2(np.random.permutation(np.resize(levels, k // 32))).repeat(32)
    a = np.empty((k // 512, 16))
    for p in range(k // 512):
        a[p, :8] = np.random.permutation(np.resize(levels, 8))
        for g in range(8):
            far = levels[np.abs(levels - a[p, g]) >= 10]
            a[p, g + 8] = far[np.random.randint(len(far))]
    return np.exp2(a.ravel()).repeat(32)


def f64(x):
    return np.asarray(x).astype(np.float64)


def striped(idx):
    return np.tile(np.asarray(idx).reshape(-1, 16).T, (8, 1)).astype(np.uint16)


def unstriped(offs):
    return offs[:16].T.reshape(-1).astype(np.int64)


E2M1 = np.array([0.0, 0.5, 1.0, 1.5, 2.0, 3.0, 4.0, 6.0, -0.0, -0.5, -1.0, -1.5, -2.0, -3.0, -4.0, -6.0])


def pack_weight(w, fmt):
    k, n = w.shape
    w = f64(np.asarray(w, np.float32).astype(ml_dtypes.bfloat16)).reshape(k // 32, 32, n)
    amax = np.abs(w).max(1)
    if fmt == "e4m3":
        byte = np.frexp(amax)[1] - 1 + 127 - 7
    else:
        mant, ex = np.frexp(amax / 6.0)
        byte = np.where(mant > 0.5, ex, ex - 1) + 127
    byte = np.clip(np.where(amax > 0, byte, 1), 1, 254)
    scaled = (w * np.exp2(127.0 - byte)[:, None, :]).reshape(k, n).astype(np.float32)
    by_word = np.ascontiguousarray(scaled.reshape(k // 512, 128, 4, n).transpose(0, 1, 3, 2))
    if fmt == "e4m3":
        words = by_word.astype(ml_dtypes.float8_e4m3fn).view(np.uint8)
    else:
        c = by_word.astype(ml_dtypes.float4_e2m1fn).view(np.uint8) & 0xF
        words = (c[..., 0::2] | (c[..., 1::2] << 4)).reshape(k // 512, 128, 2 * n)
    return np.ascontiguousarray(words), np.ascontiguousarray(byte.astype(np.uint8).reshape(k // 512, 16, n))


def unpack_weight(words, scales, fmt):
    g, _, n = scales.shape
    words = np.ascontiguousarray(words).reshape(g, 128, n, -1)
    if fmt == "e4m3":
        vals = words.view(ml_dtypes.float8_e4m3fn).astype(np.float64)
    else:
        nib = np.empty((g, 128, n, 4), np.uint8)
        nib[..., 0::2] = words & 0xF
        nib[..., 1::2] = words >> 4
        vals = E2M1[nib]
    vals = vals * np.repeat(np.exp2(scales.astype(np.float64) - 127.0), 8, axis=1)[..., None]
    return vals.transpose(0, 1, 3, 2).reshape(g * 512, n)


def bf(x):
    return np.asarray(x, np.float32).astype(ml_dtypes.bfloat16)


def planes(Y):
    r, m = Y.shape
    b = f64(bf(Y)).reshape(r // 32, 32, m)
    amax = np.abs(b).max(1)
    byte = np.clip(np.where(amax > 0, np.frexp(amax)[1] - 1 + 127 - 7, 1), 1, 254)
    codes = (b * np.exp2(127.0 - byte)[:, None, :]).reshape(r, m).astype(np.float32).astype(ml_dtypes.float8_e4m3fn).view(np.uint8)
    words = codes.reshape(r // 512, 128, 4, m).transpose(0, 1, 3, 2)
    return np.ascontiguousarray(words), np.ascontiguousarray(byte.astype(np.uint8).reshape(r // 512, 16, m))


D, T, I, Q, E, U = 512, 2048, 512, 256, 512, 512


def setup_inputs():
    n = np.random.standard_normal
    idx = np.random.permutation(T)[:I]
    idx2 = np.random.randint(0, U, I)
    fd = mx_kscale(D)
    fi = mx_kscale(I)
    ti = np.ones(T)
    ti[idx] = fi
    keysp = pack_weight(n((D, T)) / fd[:, None], "e2m1")
    return {
        "query": (n((D, Q)) * 0.4 / np.sqrt(D) * fd[:, None]).astype(np.float32),
        "keys_words": keysp[0],
        "keys_scales": keysp[1],
        "bias": (0.5 * n((Q, U))).astype(np.float32),
        "gate": (np.random.uniform(0.2, 0.8, (Q, 1))).astype(np.float32),
        "size": (np.random.uniform(0.5, 2.0, (1, I)) * fi).astype(np.float32),
        "vals": (n((E, T)) / ti).astype(np.float32),
        "offs": striped(idx),
        "offs2": striped(idx2),
    }


def reference(query, keys_words, keys_scales, bias, gate, size, vals, offs, offs2):
    idx = unstriped(offs)
    idx2 = unstriped(offs2)
    keysu = unpack_weight(keys_words, keys_scales, "e2m1")
    queryq = mxq(f64(query), 0, "e4m3")
    keysidxg = keysu[:, idx]
    a = queryq.T @ keysidxg
    s = a + f64(bias)[:, idx2]
    p = np.exp(s - np.max(s, axis=1, keepdims=True))
    r = np.exp(a - np.max(a, axis=1, keepdims=True))
    w = (f64(gate) * p / np.sum(p, axis=1, keepdims=True) + (1.0 - f64(gate)) * r / np.sum(r, axis=1, keepdims=True)) * f64(size)
    wt = w.T
    vt = f64(vals)[:, idx].T
    vtq = mxq(vt, 0, "e4m3")
    wtq = mxq(wt, 0, "e4m3")
    o = vtq.T @ wtq
    words, scales = planes(o)
    return o, words, scales

@@ -1,0 +1,270 @@
+from contextlib import ExitStack
+
+import concourse.mybir as mybir
+from concourse.masks import make_identity
+
+D, T, I, Q, E, U = 512, 2048, 512, 256, 512, 512
+FLOPS = 2 * D * Q * I + 2 * I * E * Q
+
+F32 = mybir.dt.float32
+BF16 = mybir.dt.bfloat16
+I32 = mybir.dt.int32
+U32 = mybir.dt.uint32
+U16 = mybir.dt.uint16
+U8 = mybir.dt.uint8
+FP8X4 = mybir.dt.float8_e4m3fn_x4
+FP4X4 = mybir.dt.float4_e2m1fn_x4
+ALU = mybir.AluOpType
+ACT = mybir.ActivationFunctionType
+AX = mybir.AxisListType
+
+P = 128
+PACK = 4
+HALVES = Q // P
+BIAS_WINDOW = 704
+
+
+def tile_attend_mixedbias_pl_kernel(
+    tc, query, keys_words, keys_scales, bias, gate, size, vals, offs, offs2, out_0, out_1, out_2
+):
+    nc = tc.nc
+    with ExitStack() as ctx:
+        sb = ctx.enter_context(tc.tile_pool(name="sb", bufs=1))
+        ps = ctx.enter_context(tc.psum_pool(name="ps", bufs=1))
+        ps_turn = ctx.enter_context(tc.psum_pool(name="ps_turn", bufs=2))
+
+        slots = sb.tile([P, I // 16], U16)
+        buckets = sb.tile([P, I // 16], U16)
+        key_words = sb.tile([P, T], U16, align_bytes=64)
+        key_scales = sb.tile([P, T], U8, align_bytes=64)
+        q_raw = sb.tile([P, PACK, Q], F32)
+        bias_rows = sb.tile([P, (HALVES - 1) * U + BIAS_WINDOW], F32)
+        gates = sb.tile([P, HALVES, 1], F32)
+        sizes = sb.tile([P, PACK], F32)
+        v_raw = [
+            sb.tile([P, T], F32, align_bytes=64, name="v_raw%d" % r, tag="values%d" % r) for r in range(PACK)
+        ]
+        ident = sb.tile([P, P], F32)
+        warm = sb.tile([P, 1], F32)
+        warm_out = sb.tile([P, 1], F32)
+
+        nc.gpsimd.memset(key_scales[:].bitcast(I32), 0)
+        nc.vector.memset(bias_rows[:, HALVES * U :], 0.0)
+        nc.vector.memset(warm[:], 0.0)
+        nc.scalar.activation(warm_out[:], warm[:], ACT.Exp)
+        make_identity(nc, ident[:])
+
+        nc.sync.dma_start(slots[:], offs)
+        for c in range(4):
+            nc.sync.dma_start(
+                key_scales[32 * c : 32 * c + 4, :].bitcast(I32),
+                keys_scales[0, 4 * c : 4 * c + 4, :].bitcast(I32),
+            )
+        nc.sync.dma_start(key_words[:].bitcast(I32), keys_words[0].bitcast(I32))
+        nc.sync.dma_start(q_raw[:], query.rearrange("(p j) q -> p j q", j=PACK))
+        nc.sync.dma_start(buckets[:], offs2)
+        nc.sync.dma_start(
+            bias_rows[:, : HALVES * U].rearrange("p (h u) -> p h u", h=HALVES),
+            bias.rearrange("(h p) u -> p h u", p=P),
+        )
+        vals_dealt = vals.rearrange("(p r) t -> r p t", r=PACK)
+        nc.sync.dma_start(v_raw[0][:], vals_dealt[0])
+        with nc.allow_non_contiguous_dma(reason="one gate for each partition and half"):
+            nc.sync.dma_start(gates[:], gate.rearrange("(h p) o -> p h o", p=P))
+        nc.sync.dma_start(sizes[:], size.rearrange("o (p t) -> p (o t)", t=PACK))
+        for r in range(1, PACK):
+            nc.sync.dma_start(v_raw[r][:], vals_dealt[r])
+
+        k_words = sb.tile([P, I], U16, align_bytes=64)
+        k_scales = sb.tile([P, I], U8, align_bytes=64)
+        nc.vector.tensor_copy(k_scales[:], key_scales[:].indirect(slots[:]))
+        nc.vector.tensor_copy(k_words[:], key_words[:].indirect(slots[:]))
+        q_bf = [sb.tile([P, P, PACK], BF16, align_bytes=64, name="q_bf%d" % h) for h in range(HALVES)]
+        q_codes = sb.tile([P, Q], U32, align_bytes=64)
+        q_scales = sb.tile([P, Q], U8, align_bytes=64)
+        for h in range(HALVES):
+            nc.scalar.copy(q_bf[h][:], q_raw[:, :, h * P : (h + 1) * P].rearrange("p j q -> p q j"))
+        scores = [ps.tile([P, I], F32, name="scores%d" % h) for h in range(HALVES)]
+        for h in range(HALVES):
+            cols = slice(h * P, (h + 1) * P)
+            nc.vector.quantize_mx(
+                out=q_codes[:, cols].bitcast(FP8X4),
+                scales=q_scales[:, cols],
+                in_=q_bf[h][:].rearrange("p q j -> p (q j)"),
+            )
+            nc.tensor.matmul_mx(
+                out=scores[h][:],
+                lhsT=q_codes[:, cols].bitcast(FP8X4),
+                lhsT_scale=q_scales[:, cols],
+                rhs=k_words[:].bitcast(FP4X4),
+                rhs_scale=k_scales[:],
+                start=True,
+                stop=True,
+            )
+
+        shares = sb.tile([P, HALVES, 2], F32)
+        nc.gpsimd.tensor_copy(shares[:, :, 0:1], gates[:])
+        nc.gpsimd.tensor_scalar(shares[:, :, 1:2], gates[:], -1.0, 1.0, ALU.mult, ALU.add)
+
+        w_codes = sb.tile([P, Q], U32, align_bytes=64)
+        w_scales = sb.tile([P, Q], U8, align_bytes=64)
+        v_codes = [sb.tile([P, P], U32, align_bytes=64, name="v_codes%d" % r) for r in range(PACK)]
+        v_scales = [sb.tile([P, P], U8, align_bytes=64, name="v_scales%d" % r) for r in range(PACK)]
+        v_bf = [sb.tile([P, P, PACK], BF16, align_bytes=64, name="v_bf%d" % r) for r in range(PACK)]
+        w_bf = [None] * HALVES
+        exps = [sb.tile([P, 2, PACK, P], F32, name="exps%d" % h) for h in range(HALVES)]
+        sums = [sb.tile([P, 2], F32, name="sums%d" % h) for h in range(HALVES)]
+        w_turned = [ps.tile([P, PACK, P], F32, name="w_turned%d" % h) for h in range(HALVES)]
+
+        biased = [sb.tile([P, I], F32, name="biased%d" % h) for h in range(HALVES)]
+
+        def plain_exp(h):
+            neg_max = sb.tile([P, 1], F32, name="neg_max_a%d" % h)
+            nc.vector.tensor_reduce(neg_max[:], scores[h][:], AX.X, ALU.max, negate=True)
+            nc.scalar.activation(
+                exps[h][:, 1],
+                scores[h][:].rearrange("p (s t) -> p t s", t=PACK),
+                ACT.Exp,
+                bias=neg_max[:],
+                accum_out=sums[h][:, 1:2],
+            )
+
+        def add_bias(h):
+            slot_bias = sb.tile([P, I], F32, name="slot_bias")
+            nc.vector.tensor_copy(
+                slot_bias[:], bias_rows[:, h * U : h * U + BIAS_WINDOW].indirect(buckets[:])
+            )
+            return slot_bias
+
+        def biased_exp(h):
+            neg_max = sb.tile([P, 1], F32, name="neg_max_s%d" % h)
+            nc.vector.tensor_reduce(neg_max[:], biased[h][:], AX.X, ALU.max, negate=True)
+            nc.scalar.activation(
+                exps[h][:, 0].rearrange("p t s -> p s t"),
+                biased[h][:].rearrange("p (s t) -> p s t", t=PACK),
+                ACT.Exp,
+                bias=neg_max[:],
+                accum_out=sums[h][:, 0:1],
+            )
+
+        def turn_weights(h):
+            inv = sb.tile([P, 2], F32, name="inv%d" % h)
+            coef = sb.tile([P, 2], F32, name="coef%d" % h)
+            parts = sb.tile([P, 2, PACK, P], F32, name="parts%d" % h)
+            nc.vector.reciprocal(inv[:], sums[h][:])
+            nc.vector.tensor_tensor(coef[:], inv[:], shares[:, h, :], ALU.mult)
+            for k in range(2):
+                nc.scalar.activation(parts[:, k], exps[h][:, k], ACT.Copy, scale=coef[:, k : k + 1])
+                for t in range(PACK):
+                    nc.tensor.matmul(
+                        w_turned[h][:, t, :],
+                        parts[:, k, t, :],
+                        ident[:],
+                        start=(k == 0 and t == 0),
+                        stop=(k == 1 and t == PACK - 1),
+                        is_transpose=True,
+                    )
+
+        def round_weights(h, after):
+            w_bf[h] = sb.tile([P, P, PACK], BF16, align_bytes=64, name="w_bf%d" % h, tag="values%d" % after)
+            nc.vector.tensor_tensor(
+                w_bf[h][:],
+                w_turned[h][:].rearrange("p t q -> p q t"),
+                sizes[:].unsqueeze(1).to_broadcast([P, P, PACK]),
+                ALU.mult,
+            )
+
+        def quantise_weights(h):
+            cols = slice(h * P, (h + 1) * P)
+            nc.vector.quantize_mx(
+                out=w_codes[:, cols].bitcast(FP8X4),
+                scales=w_scales[:, cols],
+                in_=w_bf[h][:].rearrange("p q t -> p (q t)"),
+            )
+
+        def gather_values(r):
+            listed = sb.tile([P, I], BF16, name="listed%d" % r)
+            nc.vector.tensor_copy(listed[:], v_raw[r][:].indirect(slots[:]))
+            pairs = listed[:].bitcast(F32)
+            turned = ps_turn.tile([P, 2, P], F32, name="turned")
+            for u in range(2):
+                nc.tensor.transpose(turned[:, u, :], pairs[:, u::2], ident[:])
+            nc.scalar.copy(
+                v_bf[r][:].rearrange("p m t -> p (m t)").bitcast(F32).rearrange("p (m u) -> p m u", u=2),
+                turned[:].rearrange("p u m -> p m u"),
+            )
+
+        def quantise_values(r):
+            nc.vector.quantize_mx(
+                out=v_codes[r][:].bitcast(FP8X4),
+                scales=v_scales[r][:],
+                in_=v_bf[r][:].rearrange("p m t -> p (m t)"),
+            )
+
+        result = [ps.tile([P, PACK, P], F32, name="result%d" % h) for h in range(HALVES)]
+
+        def product(r, h):
+            cols = slice(h * P, (h + 1) * P)
+            nc.tensor.matmul_mx(
+                out=result[h][:, r, :],
+                lhsT=v_codes[r][:].bitcast(FP8X4),
+                lhsT_scale=v_scales[r][:],
+                rhs=w_codes[:, cols].bitcast(FP8X4),
+                rhs_scale=w_scales[:, cols],
+                start=True,
+                stop=True,
+            )
+
+        b0 = add_bias(0)
+        plain_exp(0)
+        nc.vector.tensor_tensor(biased[0][:], scores[0][:], b0[:], ALU.add)
+        plain_exp(1)
+        biased_exp(0)
+        b1 = add_bias(1)
+        nc.vector.tensor_tensor(biased[1][:], scores[1][:], b1[:], ALU.add)
+        turn_weights(0)
+        biased_exp(1)
+        gather_values(0)
+        turn_weights(1)
+        gather_values(1)
+        quantise_values(0)
+        round_weights(0, 1)
+        gather_values(2)
+        quantise_weights(0)
+        quantise_values(1)
+        gather_values(3)
+        round_weights(1, 3)
+        quantise_values(2)
+        quantise_weights(1)
+        quantise_values(3)
+
+        out_rows = out_0.rearrange("(p r) q -> p r q", r=PACK)
+        o_early = sb.tile([P, PACK - 1, P], F32)
+        o_late = sb.tile([P, P], F32)
+        o_second = sb.tile([P, PACK, P], F32)
+        for r in range(PACK - 1):
+            product(r, 0)
+        nc.scalar.copy(o_early[:], result[0][:, : PACK - 1, :])
+        nc.sync.dma_start(out_rows[:, : PACK - 1, :P], o_early[:])
+        for r in range(PACK):
+            product(r, 1)
+        product(PACK - 1, 0)
+        o_bf = sb.tile([P, Q, PACK], BF16, align_bytes=64)
+        o_codes = sb.tile([P, Q], U32, align_bytes=64)
+        o_scales = sb.tile([P, Q], U8, align_bytes=64)
+        nc.vector.tensor_copy(o_bf[:, P:, :], result[1][:].rearrange("p r q -> p q r"))
+        nc.scalar.copy(o_bf[:, :P, :], result[0][:].rearrange("p r q -> p q r"))
+        nc.vector.quantize_mx(
+            out=o_codes[:].bitcast(FP8X4), scales=o_scales[:], in_=o_bf[:].rearrange("p q r -> p (q r)")
+        )
+        nc.scalar.copy(o_second[:], result[1][:])
+        nc.scalar.dma_start(out_rows[:, :, P:], o_second[:])
+        nc.scalar.copy(o_late[:], result[0][:, PACK - 1, :])
+        nc.scalar.dma_start(out_rows[:, PACK - 1, :P], o_late[:])
+        nc.sync.dma_start(out_1[0].rearrange("p q r -> p (q r)").bitcast(I32), o_codes[:].bitcast(I32))
+        for c in range(4):
+            queue = nc.sync if c < 2 else nc.scalar
+            queue.dma_start(
+                out_2[0, 4 * c : 4 * c + 4, :].bitcast(I32),
+                o_scales[32 * c : 32 * c + 4, :].bitcast(I32),
+            )

@@ -22,6 +22,7 @@ P = 128
 PACK = 4
 HALVES = Q // P
 BIAS_WINDOW = 704
+ROW_BYTES = 4 * T
 
 
 def tile_attend_mixedbias_pl_kernel(
@@ -30,6 +31,7 @@ def tile_attend_mixedbias_pl_kernel(
     nc = tc.nc
     with ExitStack() as ctx:
         sb = ctx.enter_context(tc.tile_pool(name="sb", bufs=1))
+        placed = ctx.enter_context(tc.tile_pool(name="placed", bufs=1))
         ps = ctx.enter_context(tc.psum_pool(name="ps", bufs=1))
         ps_turn = ctx.enter_context(tc.psum_pool(name="ps_turn", bufs=2))
 
@@ -38,22 +40,25 @@ def tile_attend_mixedbias_pl_kernel(
         key_words = sb.tile([P, T], U16, align_bytes=64)
         key_scales = sb.tile([P, T], U8, align_bytes=64)
         q_raw = sb.tile([P, PACK, Q], F32)
-        bias_rows = sb.tile([P, (HALVES - 1) * U + BIAS_WINDOW], F32)
+        bias_rows = [sb.tile([P, BIAS_WINDOW], F32, name="bias_rows%d" % h) for h in range(HALVES)]
         gates = sb.tile([P, HALVES, 1], F32)
         sizes = sb.tile([P, PACK], F32)
         v_raw = [
-            sb.tile([P, T], F32, align_bytes=64, name="v_raw%d" % r, tag="values%d" % r) for r in range(PACK)
+            placed.tile([P, T], F32, align_bytes=64, name="v_raw%d" % r, offset=r * ROW_BYTES) for r in range(PACK)
         ]
         ident = sb.tile([P, P], F32)
         warm = sb.tile([P, 1], F32)
         warm_out = sb.tile([P, 1], F32)
 
         nc.gpsimd.memset(key_scales[:].bitcast(I32), 0)
-        nc.vector.memset(bias_rows[:, HALVES * U :], 0.0)
+        for h in range(HALVES):
+            nc.vector.memset(bias_rows[h][:, U:], 0.0)
         nc.vector.memset(warm[:], 0.0)
         nc.scalar.activation(warm_out[:], warm[:], ACT.Exp)
         make_identity(nc, ident[:])
 
+        nc.sync.dma_start(buckets[:], offs2)
+        nc.sync.dma_start(bias_rows[0][:, :U], bias[:P, :])
         nc.sync.dma_start(slots[:], offs)
         for c in range(4):
             nc.sync.dma_start(
@@ -62,11 +67,7 @@ def tile_attend_mixedbias_pl_kernel(
             )
         nc.sync.dma_start(key_words[:].bitcast(I32), keys_words[0].bitcast(I32))
         nc.sync.dma_start(q_raw[:], query.rearrange("(p j) q -> p j q", j=PACK))
-        nc.sync.dma_start(buckets[:], offs2)
-        nc.sync.dma_start(
-            bias_rows[:, : HALVES * U].rearrange("p (h u) -> p h u", h=HALVES),
-            bias.rearrange("(h p) u -> p h u", p=P),
-        )
+        nc.sync.dma_start(bias_rows[1][:, :U], bias[P:, :])
         vals_dealt = vals.rearrange("(p r) t -> r p t", r=PACK)
         nc.sync.dma_start(v_raw[0][:], vals_dealt[0])
         with nc.allow_non_contiguous_dma(reason="one gate for each partition and half"):
@@ -75,16 +76,22 @@ def tile_attend_mixedbias_pl_kernel(
         for r in range(1, PACK):
             nc.sync.dma_start(v_raw[r][:], vals_dealt[r])
 
+        slot_bias = [sb.tile([P, I], F32, name="slot_bias0")]
         k_words = sb.tile([P, I], U16, align_bytes=64)
         k_scales = sb.tile([P, I], U8, align_bytes=64)
-        nc.vector.tensor_copy(k_scales[:], key_scales[:].indirect(slots[:]))
-        nc.vector.tensor_copy(k_words[:], key_words[:].indirect(slots[:]))
-        q_bf = [sb.tile([P, P, PACK], BF16, align_bytes=64, name="q_bf%d" % h) for h in range(HALVES)]
+        q_bf = [
+            placed.tile([P, P, PACK], BF16, align_bytes=64, name="q_bf%d" % h, offset=PACK * ROW_BYTES + 1024 * h)
+            for h in range(HALVES)
+        ]
         q_codes = sb.tile([P, Q], U32, align_bytes=64)
         q_scales = sb.tile([P, Q], U8, align_bytes=64)
+        scores = [ps.tile([P, I], F32, name="scores%d" % h, tag="bank%d" % h) for h in range(HALVES)]
+
+        nc.vector.tensor_copy(slot_bias[0][:], bias_rows[0][:].indirect(buckets[:]))
+        nc.vector.tensor_copy(k_scales[:], key_scales[:].indirect(slots[:]))
+        nc.vector.tensor_copy(k_words[:], key_words[:].indirect(slots[:]))
         for h in range(HALVES):
             nc.scalar.copy(q_bf[h][:], q_raw[:, :, h * P : (h + 1) * P].rearrange("p j q -> p q j"))
-        scores = [ps.tile([P, I], F32, name="scores%d" % h) for h in range(HALVES)]
         for h in range(HALVES):
             cols = slice(h * P, (h + 1) * P)
             nc.vector.quantize_mx(
@@ -101,72 +108,75 @@ def tile_attend_mixedbias_pl_kernel(
                 start=True,
                 stop=True,
             )
+        slot_bias.append(placed.tile([P, I], F32, align_bytes=64, name="slot_bias1", offset=PACK * ROW_BYTES))
+        nc.vector.tensor_copy(slot_bias[1][:], bias_rows[1][:].indirect(buckets[:]))
 
-        shares = sb.tile([P, HALVES, 2], F32)
-        nc.gpsimd.tensor_copy(shares[:, :, 0:1], gates[:])
-        nc.gpsimd.tensor_scalar(shares[:, :, 1:2], gates[:], -1.0, 1.0, ALU.mult, ALU.add)
+        rest = sb.tile([P, HALVES, 1], F32)
+        nc.gpsimd.tensor_scalar(rest[:], gates[:], -1.0, 1.0, ALU.mult, ALU.add)
+        shares = (gates, rest)
 
+        last = (PACK - 1) * ROW_BYTES
+        w_bf = [None] * HALVES
         w_codes = sb.tile([P, Q], U32, align_bytes=64)
         w_scales = sb.tile([P, Q], U8, align_bytes=64)
-        v_codes = [sb.tile([P, P], U32, align_bytes=64, name="v_codes%d" % r) for r in range(PACK)]
-        v_scales = [sb.tile([P, P], U8, align_bytes=64, name="v_scales%d" % r) for r in range(PACK)]
-        v_bf = [sb.tile([P, P, PACK], BF16, align_bytes=64, name="v_bf%d" % r) for r in range(PACK)]
-        w_bf = [None] * HALVES
+        v_bf = [sb.tile([P, 2, P, PACK], BF16, align_bytes=64, name="v_bf%d" % g) for g in range(2)]
+        v_codes = [None] * 2
+        v_scales = [sb.tile([P, 2 * P], U8, align_bytes=64, name="v_scales%d" % g) for g in range(2)]
         exps = [sb.tile([P, 2, PACK, P], F32, name="exps%d" % h) for h in range(HALVES)]
-        sums = [sb.tile([P, 2], F32, name="sums%d" % h) for h in range(HALVES)]
+        sums = sb.tile([P, HALVES, 2], F32)
+        inv = sb.tile([P, HALVES, 2], F32)
+        biased = [sb.tile([P, I], F32, name="biased%d" % h) for h in range(HALVES)]
+        neg_max_a = [sb.tile([P, 1], F32, name="neg_max_a%d" % h) for h in range(HALVES)]
+        neg_max_s = [sb.tile([P, 1], F32, name="neg_max_s%d" % h) for h in range(HALVES)]
+        parts = [sb.tile([P, 2, PACK, P], F32, name="parts%d" % h) for h in range(HALVES)]
+        coef = [sb.tile([P, 2], F32, name="coef%d" % h) for h in range(HALVES)]
         w_turned = [ps.tile([P, PACK, P], F32, name="w_turned%d" % h) for h in range(HALVES)]
 
-        biased = [sb.tile([P, I], F32, name="biased%d" % h) for h in range(HALVES)]
+        def plain_max(h):
+            nc.vector.tensor_reduce(neg_max_a[h][:], scores[h][:], AX.X, ALU.max, negate=True)
 
-        def plain_exp(h):
-            neg_max = sb.tile([P, 1], F32, name="neg_max_a%d" % h)
-            nc.vector.tensor_reduce(neg_max[:], scores[h][:], AX.X, ALU.max, negate=True)
+        def add_bias(h):
+            nc.vector.tensor_tensor(biased[h][:], scores[h][:], slot_bias[h][:], ALU.add)
             nc.scalar.activation(
                 exps[h][:, 1],
                 scores[h][:].rearrange("p (s t) -> p t s", t=PACK),
                 ACT.Exp,
-                bias=neg_max[:],
-                accum_out=sums[h][:, 1:2],
+                bias=neg_max_a[h][:],
+                accum_out=sums[:, h, 1:2],
             )
-
-        def add_bias(h):
-            slot_bias = sb.tile([P, I], F32, name="slot_bias")
-            nc.vector.tensor_copy(
-                slot_bias[:], bias_rows[:, h * U : h * U + BIAS_WINDOW].indirect(buckets[:])
-            )
-            return slot_bias
 
         def biased_exp(h):
-            neg_max = sb.tile([P, 1], F32, name="neg_max_s%d" % h)
-            nc.vector.tensor_reduce(neg_max[:], biased[h][:], AX.X, ALU.max, negate=True)
+            nc.vector.tensor_reduce(neg_max_s[h][:], biased[h][:], AX.X, ALU.max, negate=True)
             nc.scalar.activation(
                 exps[h][:, 0].rearrange("p t s -> p s t"),
                 biased[h][:].rearrange("p (s t) -> p s t", t=PACK),
                 ACT.Exp,
-                bias=neg_max[:],
-                accum_out=sums[h][:, 0:1],
+                bias=neg_max_s[h][:],
+                accum_out=sums[:, h, 0:1],
             )
 
-        def turn_weights(h):
-            inv = sb.tile([P, 2], F32, name="inv%d" % h)
-            coef = sb.tile([P, 2], F32, name="coef%d" % h)
-            parts = sb.tile([P, 2, PACK, P], F32, name="parts%d" % h)
-            nc.vector.reciprocal(inv[:], sums[h][:])
-            nc.vector.tensor_tensor(coef[:], inv[:], shares[:, h, :], ALU.mult)
+        def coefficients(h):
             for k in range(2):
-                nc.scalar.activation(parts[:, k], exps[h][:, k], ACT.Copy, scale=coef[:, k : k + 1])
-                for t in range(PACK):
-                    nc.tensor.matmul(
-                        w_turned[h][:, t, :],
-                        parts[:, k, t, :],
-                        ident[:],
-                        start=(k == 0 and t == 0),
-                        stop=(k == 1 and t == PACK - 1),
-                        is_transpose=True,
-                    )
+                nc.scalar.activation(
+                    coef[h][:, k : k + 1], inv[:, h, k : k + 1], ACT.Copy, scale=shares[k][:, h, :]
+                )
 
-        def round_weights(h, after):
-            w_bf[h] = sb.tile([P, P, PACK], BF16, align_bytes=64, name="w_bf%d" % h, tag="values%d" % after)
+        def turn_part(h, k):
+            nc.scalar.activation(parts[h][:, k], exps[h][:, k], ACT.Copy, scale=coef[h][:, k : k + 1])
+            for t in range(PACK):
+                nc.tensor.matmul(
+                    w_turned[h][:, t, :],
+                    parts[h][:, k, t, :],
+                    ident[:],
+                    start=(k == 0 and t == 0),
+                    stop=(k == 1 and t == PACK - 1),
+                    is_transpose=True,
+                )
+
+        def round_weights(h):
+            w_bf[h] = placed.tile(
+                [P, P, PACK], BF16, align_bytes=64, name="w_bf%d" % h, offset=last + 1024 * h
+            )
             nc.vector.tensor_tensor(
                 w_bf[h][:],
                 w_turned[h][:].rearrange("p t q -> p q t"),
@@ -182,88 +192,93 @@ def tile_attend_mixedbias_pl_kernel(
                 in_=w_bf[h][:].rearrange("p q t -> p (q t)"),
             )
 
+        listed = [sb.tile([P, I], BF16, name="listed%d" % r) for r in range(PACK)]
+
         def gather_values(r):
-            listed = sb.tile([P, I], BF16, name="listed%d" % r)
-            nc.vector.tensor_copy(listed[:], v_raw[r][:].indirect(slots[:]))
-            pairs = listed[:].bitcast(F32)
+            nc.vector.tensor_copy(listed[r][:], v_raw[r][:].indirect(slots[:]))
+
+        def turn_values(r):
+            pairs = listed[r][:].bitcast(F32)
             turned = ps_turn.tile([P, 2, P], F32, name="turned")
             for u in range(2):
                 nc.tensor.transpose(turned[:, u, :], pairs[:, u::2], ident[:])
             nc.scalar.copy(
-                v_bf[r][:].rearrange("p m t -> p (m t)").bitcast(F32).rearrange("p (m u) -> p m u", u=2),
+                v_bf[r // 2][:, r % 2].rearrange("p m t -> p (m t)").bitcast(F32).rearrange("p (m u) -> p m u", u=2),
                 turned[:].rearrange("p u m -> p m u"),
             )
 
-        def quantise_values(r):
+        def quantise_values(g):
+            v_codes[g] = placed.tile(
+                [P, 2 * P], U32, align_bytes=64, name="v_codes%d" % g, offset=last + 2048 + 1024 * g
+            )
             nc.vector.quantize_mx(
-                out=v_codes[r][:].bitcast(FP8X4),
-                scales=v_scales[r][:],
-                in_=v_bf[r][:].rearrange("p m t -> p (m t)"),
+                out=v_codes[g][:].bitcast(FP8X4),
+                scales=v_scales[g][:],
+                in_=v_bf[g][:].rearrange("p a m t -> p (a m t)"),
             )
 
-        result = [ps.tile([P, PACK, P], F32, name="result%d" % h) for h in range(HALVES)]
-
-        def product(r, h):
+        def product(out, r, h):
             cols = slice(h * P, (h + 1) * P)
+            feats = slice((r % 2) * P, (r % 2 + 1) * P)
             nc.tensor.matmul_mx(
-                out=result[h][:, r, :],
-                lhsT=v_codes[r][:].bitcast(FP8X4),
-                lhsT_scale=v_scales[r][:],
+                out=out,
+                lhsT=v_codes[r // 2][:, feats].bitcast(FP8X4),
+                lhsT_scale=v_scales[r // 2][:, feats],
                 rhs=w_codes[:, cols].bitcast(FP8X4),
                 rhs_scale=w_scales[:, cols],
                 start=True,
                 stop=True,
             )
 
-        b0 = add_bias(0)
-        plain_exp(0)
-        nc.vector.tensor_tensor(biased[0][:], scores[0][:], b0[:], ALU.add)
-        plain_exp(1)
-        biased_exp(0)
-        b1 = add_bias(1)
-        nc.vector.tensor_tensor(biased[1][:], scores[1][:], b1[:], ALU.add)
-        turn_weights(0)
-        biased_exp(1)
+        for h in range(HALVES):
+            plain_max(h)
+            add_bias(h)
+        for h in range(HALVES):
+            biased_exp(h)
         gather_values(0)
-        turn_weights(1)
+        nc.vector.reciprocal(inv[:], sums[:])
+        coefficients(0)
+        turn_part(0, 0)
+        coefficients(1)
+        turn_part(0, 1)
+        turn_values(0)
         gather_values(1)
-        quantise_values(0)
-        round_weights(0, 1)
+        turn_part(1, 0)
+        turn_values(1)
         gather_values(2)
-        quantise_weights(0)
-        quantise_values(1)
+        turn_part(1, 1)
+        turn_values(2)
         gather_values(3)
-        round_weights(1, 3)
-        quantise_values(2)
+        turn_values(3)
+        round_weights(0)
+        quantise_values(0)
+        quantise_weights(0)
+        round_weights(1)
+        quantise_values(1)
         quantise_weights(1)
-        quantise_values(3)
 
         out_rows = out_0.rearrange("(p r) q -> p r q", r=PACK)
-        o_early = sb.tile([P, PACK - 1, P], F32)
-        o_late = sb.tile([P, P], F32)
-        o_second = sb.tile([P, PACK, P], F32)
-        for r in range(PACK - 1):
-            product(r, 0)
-        nc.scalar.copy(o_early[:], result[0][:, : PACK - 1, :])
-        nc.sync.dma_start(out_rows[:, : PACK - 1, :P], o_early[:])
-        for r in range(PACK):
-            product(r, 1)
-        product(PACK - 1, 0)
-        o_bf = sb.tile([P, Q, PACK], BF16, align_bytes=64)
+        o_f32 = [sb.tile([P, PACK, P], F32, name="o_f32_%d" % h) for h in range(HALVES)]
+        o_bf = [sb.tile([P, P, PACK], BF16, align_bytes=64, name="o_bf%d" % h) for h in range(HALVES)]
         o_codes = sb.tile([P, Q], U32, align_bytes=64)
         o_scales = sb.tile([P, Q], U8, align_bytes=64)
-        nc.vector.tensor_copy(o_bf[:, P:, :], result[1][:].rearrange("p r q -> p q r"))
-        nc.scalar.copy(o_bf[:, :P, :], result[0][:].rearrange("p r q -> p q r"))
-        nc.vector.quantize_mx(
-            out=o_codes[:].bitcast(FP8X4), scales=o_scales[:], in_=o_bf[:].rearrange("p q r -> p (q r)")
-        )
-        nc.scalar.copy(o_second[:], result[1][:])
-        nc.scalar.dma_start(out_rows[:, :, P:], o_second[:])
-        nc.scalar.copy(o_late[:], result[0][:, PACK - 1, :])
-        nc.scalar.dma_start(out_rows[:, PACK - 1, :P], o_late[:])
+        for h in range(HALVES):
+            cols = slice(h * P, (h + 1) * P)
+            for g in range(2):
+                result = ps.tile([P, 2, P], F32, name="result%d%d" % (h, g), tag="bank%d" % (2 * h + g))
+                for a in range(2):
+                    product(result[:, a, :], 2 * g + a, h)
+                nc.scalar.copy(o_f32[h][:, 2 * g : 2 * g + 2, :], result[:])
+            nc.sync.dma_start(out_rows[:, :, cols], o_f32[h][:])
+            nc.vector.tensor_copy(o_bf[h][:], o_f32[h][:].rearrange("p r q -> p q r"))
+            nc.vector.quantize_mx(
+                out=o_codes[:, cols].bitcast(FP8X4),
+                scales=o_scales[:, cols],
+                in_=o_bf[h][:].rearrange("p q r -> p (q r)"),
+            )
         nc.sync.dma_start(out_1[0].rearrange("p q r -> p (q r)").bitcast(I32), o_codes[:].bitcast(I32))
         for c in range(4):
-            queue = nc.sync if c < 2 else nc.scalar
+            queue = nc.sync if c < 1 else nc.scalar
             queue.dma_start(
                 out_2[0, 4 * c : 4 * c + 4, :].bitcast(I32),
                 o_scales[32 * c : 32 * c + 4, :].bitcast(I32),

@@ -123,8 +123,8 @@ def tile_attend_mixedbias_pl_kernel(
         v_codes = [None] * 2
         v_scales = [sb.tile([P, 2 * P], U8, align_bytes=64, name="v_scales%d" % g) for g in range(2)]
         exps = [sb.tile([P, 2, PACK, P], F32, name="exps%d" % h) for h in range(HALVES)]
-        sums = sb.tile([P, HALVES, 2], F32)
-        inv = sb.tile([P, HALVES, 2], F32)
+        sums = sb.tile([P, 2, HALVES], F32)
+        inv = sb.tile([P, 2, HALVES], F32)
         biased = [sb.tile([P, I], F32, name="biased%d" % h) for h in range(HALVES)]
         neg_max_a = [sb.tile([P, 1], F32, name="neg_max_a%d" % h) for h in range(HALVES)]
         neg_max_s = [sb.tile([P, 1], F32, name="neg_max_s%d" % h) for h in range(HALVES)]
@@ -142,7 +142,7 @@ def tile_attend_mixedbias_pl_kernel(
                 scores[h][:].rearrange("p (s t) -> p t s", t=PACK),
                 ACT.Exp,
                 bias=neg_max_a[h][:],
-                accum_out=sums[:, h, 1:2],
+                accum_out=sums[:, 1, h : h + 1],
             )
 
         def biased_exp(h):
@@ -152,24 +152,21 @@ def tile_attend_mixedbias_pl_kernel(
                 biased[h][:].rearrange("p (s t) -> p s t", t=PACK),
                 ACT.Exp,
                 bias=neg_max_s[h][:],
-                accum_out=sums[:, h, 0:1],
+                accum_out=sums[:, 0, h : h + 1],
             )
 
-        def coefficients(h):
-            for k in range(2):
-                nc.scalar.activation(
-                    coef[h][:, k : k + 1], inv[:, h, k : k + 1], ACT.Copy, scale=shares[k][:, h, :]
-                )
+        def scale_part(h, k):
+            nc.scalar.activation(coef[h][:, k : k + 1], inv[:, k, h : h + 1], ACT.Copy, scale=shares[k][:, h, :])
+            nc.scalar.activation(parts[h][:, k], exps[h][:, k], ACT.Copy, scale=coef[h][:, k : k + 1])
 
         def turn_part(h, k):
-            nc.scalar.activation(parts[h][:, k], exps[h][:, k], ACT.Copy, scale=coef[h][:, k : k + 1])
             for t in range(PACK):
                 nc.tensor.matmul(
                     w_turned[h][:, t, :],
                     parts[h][:, k, t, :],
                     ident[:],
-                    start=(k == 0 and t == 0),
-                    stop=(k == 1 and t == PACK - 1),
+                    start=(k == 1 and t == 0),
+                    stop=(k == 0 and t == PACK - 1),
                     is_transpose=True,
                 )
 
@@ -233,23 +230,28 @@ def tile_attend_mixedbias_pl_kernel(
         for h in range(HALVES):
             plain_max(h)
             add_bias(h)
+        nc.vector.reciprocal(inv[:, 1, 0:1], sums[:, 1, 0:1])
+        nc.gpsimd.tensor_scalar(
+            parts[0][:, 1], exps[0][:, 1], inv[:, 1, 0:1], shares[1][:, 0, :], ALU.mult, ALU.mult
+        )
+        turn_part(0, 1)
         for h in range(HALVES):
             biased_exp(h)
+        nc.vector.reciprocal(inv[:, 1, 1:2], sums[:, 1, 1:2])
+        scale_part(1, 1)
         gather_values(0)
-        nc.vector.reciprocal(inv[:], sums[:])
-        coefficients(0)
-        turn_part(0, 0)
-        coefficients(1)
-        turn_part(0, 1)
+        nc.vector.reciprocal(inv[:, 0, :], sums[:, 0, :])
+        scale_part(0, 0)
         turn_values(0)
-        gather_values(1)
-        turn_part(1, 0)
-        turn_values(1)
-        gather_values(2)
         turn_part(1, 1)
-        turn_values(2)
-        gather_values(3)
-        turn_values(3)
+        turn_part(0, 0)
+        gather_values(1)
+        scale_part(1, 0)
+        turn_values(1)
+        turn_part(1, 0)
+        for r in range(2, PACK):
+            gather_values(r)
+            turn_values(r)
         round_weights(0)
         quantise_values(0)
         quantise_weights(0)

@@ -62,11 +62,11 @@ def tile_attend_mixedbias_pl_kernel(
         nc.sync.dma_start(slots[:], offs)
         for c in range(4):
             nc.sync.dma_start(
-                key_scales[32 * c : 32 * c + 4, :].bitcast(I32),
-                keys_scales[0, 4 * c : 4 * c + 4, :].bitcast(I32),
+                key_scales[c:P:32, :].bitcast(I32),
+                keys_scales[0, c:16:4, :].bitcast(I32),
             )
-        nc.sync.dma_start(key_words[:].bitcast(I32), keys_words[0].bitcast(I32))
         nc.sync.dma_start(q_raw[:], query.rearrange("(p j) q -> p j q", j=PACK))
+        nc.sync.dma_start(key_words[:].bitcast(I32), keys_words[0].bitcast(I32))
         nc.sync.dma_start(bias_rows[1][:, :U], bias[P:, :])
         vals_dealt = vals.rearrange("(p r) t -> r p t", r=PACK)
         nc.sync.dma_start(v_raw[0][:], vals_dealt[0])
@@ -76,13 +76,10 @@ def tile_attend_mixedbias_pl_kernel(
         for r in range(1, PACK):
             nc.sync.dma_start(v_raw[r][:], vals_dealt[r])
 
-        slot_bias = [sb.tile([P, I], F32, name="slot_bias0")]
+        slot_bias = [sb.tile([P, I], F32, name="slot_bias%d" % h) for h in range(HALVES)]
         k_words = sb.tile([P, I], U16, align_bytes=64)
         k_scales = sb.tile([P, I], U8, align_bytes=64)
-        q_bf = [
-            placed.tile([P, P, PACK], BF16, align_bytes=64, name="q_bf%d" % h, offset=PACK * ROW_BYTES + 1024 * h)
-            for h in range(HALVES)
-        ]
+        q_bf = [sb.tile([P, P, PACK], BF16, align_bytes=64, name="q_bf%d" % h) for h in range(HALVES)]
         q_codes = sb.tile([P, Q], U32, align_bytes=64)
         q_scales = sb.tile([P, Q], U8, align_bytes=64)
         scores = [ps.tile([P, I], F32, name="scores%d" % h, tag="bank%d" % h) for h in range(HALVES)]
@@ -108,7 +105,6 @@ def tile_attend_mixedbias_pl_kernel(
                 start=True,
                 stop=True,
             )
-        slot_bias.append(placed.tile([P, I], F32, align_bytes=64, name="slot_bias1", offset=PACK * ROW_BYTES))
         nc.vector.tensor_copy(slot_bias[1][:], bias_rows[1][:].indirect(buckets[:]))
 
         rest = sb.tile([P, HALVES, 1], F32)
@@ -282,6 +278,6 @@ def tile_attend_mixedbias_pl_kernel(
         for c in range(4):
             queue = nc.sync if c < 1 else nc.scalar
             queue.dma_start(
-                out_2[0, 4 * c : 4 * c + 4, :].bitcast(I32),
-                o_scales[32 * c : 32 * c + 4, :].bitcast(I32),
+                out_2[0, c:16:4, :].bitcast(I32),
+                o_scales[c:P:32, :].bitcast(I32),
             )

@@ -227,12 +227,12 @@ def tile_attend_mixedbias_pl_kernel(
             plain_max(h)
             add_bias(h)
         nc.vector.reciprocal(inv[:, 1, 0:1], sums[:, 1, 0:1])
-        nc.gpsimd.tensor_scalar(
+        for h in range(HALVES):
+            biased_exp(h)
+        nc.vector.tensor_scalar(
             parts[0][:, 1], exps[0][:, 1], inv[:, 1, 0:1], shares[1][:, 0, :], ALU.mult, ALU.mult
         )
         turn_part(0, 1)
-        for h in range(HALVES):
-            biased_exp(h)
         nc.vector.reciprocal(inv[:, 1, 1:2], sums[:, 1, 1:2])
         scale_part(1, 1)
         gather_values(0)
@@ -274,9 +274,11 @@ def tile_attend_mixedbias_pl_kernel(
                 scales=o_scales[:, cols],
                 in_=o_bf[h][:].rearrange("p q r -> p (q r)"),
             )
-        nc.sync.dma_start(out_1[0].rearrange("p q r -> p (q r)").bitcast(I32), o_codes[:].bitcast(I32))
+            nc.sync.dma_start(
+                out_1[0].rearrange("p q r -> p (q r)").bitcast(I32)[:, cols], o_codes[:, cols].bitcast(I32)
+            )
         for c in range(4):
-            queue = nc.sync if c < 1 else nc.scalar
+            queue = nc.sync if c < 2 else nc.scalar
             queue.dma_start(
                 out_2[0, c:16:4, :].bitcast(I32),
                 o_scales[c:P:32, :].bitcast(I32),

@@ -37,14 +37,14 @@ def tile_attend_mixedbias_pl_kernel(
 
         slots = sb.tile([P, I // 16], U16)
         buckets = sb.tile([P, I // 16], U16)
-        key_words = sb.tile([P, T], U16, align_bytes=64)
-        key_scales = sb.tile([P, T], U8, align_bytes=64)
-        q_raw = sb.tile([P, PACK, Q], F32)
-        bias_rows = [sb.tile([P, BIAS_WINDOW], F32, name="bias_rows%d" % h) for h in range(HALVES)]
+        key_words = sb.tile([P, T], U16, align_bytes=256)
+        key_scales = sb.tile([P, T], U8, align_bytes=256)
+        q_raw = sb.tile([P, PACK, Q], F32, align_bytes=256)
+        bias_rows = [sb.tile([P, BIAS_WINDOW], F32, align_bytes=256, name="bias_rows%d" % h) for h in range(HALVES)]
         gates = sb.tile([P, HALVES, 1], F32)
         sizes = sb.tile([P, PACK], F32)
         v_raw = [
-            placed.tile([P, T], F32, align_bytes=64, name="v_raw%d" % r, offset=r * ROW_BYTES) for r in range(PACK)
+            placed.tile([P, T], F32, align_bytes=256, name="v_raw%d" % r, offset=r * ROW_BYTES) for r in range(PACK)
         ]
         ident = sb.tile([P, P], F32)
         warm = sb.tile([P, 1], F32)
@@ -115,9 +115,11 @@ def tile_attend_mixedbias_pl_kernel(
         w_bf = [None] * HALVES
         w_codes = sb.tile([P, Q], U32, align_bytes=64)
         w_scales = sb.tile([P, Q], U8, align_bytes=64)
-        v_bf = [sb.tile([P, 2, P, PACK], BF16, align_bytes=64, name="v_bf%d" % g) for g in range(2)]
-        v_codes = [None] * 2
-        v_scales = [sb.tile([P, 2 * P], U8, align_bytes=64, name="v_scales%d" % g) for g in range(2)]
+        v_bf_pair = sb.tile([P, 2, P * PACK], BF16, align_bytes=64)
+        v_bf = [v_bf_pair[:, 0, :], v_bf_pair[:, 1, :]] + [
+            sb.tile([P, P * PACK], BF16, align_bytes=64, name="v_bf%d" % r)[:] for r in range(2, PACK)
+        ]
+        v_scales = sb.tile([P, E], U8, align_bytes=64)
         exps = [sb.tile([P, 2, PACK, P], F32, name="exps%d" % h) for h in range(HALVES)]
         sums = sb.tile([P, 2, HALVES], F32)
         inv = sb.tile([P, 2, HALVES], F32)
@@ -196,27 +198,21 @@ def tile_attend_mixedbias_pl_kernel(
             for u in range(2):
                 nc.tensor.transpose(turned[:, u, :], pairs[:, u::2], ident[:])
             nc.scalar.copy(
-                v_bf[r // 2][:, r % 2].rearrange("p m t -> p (m t)").bitcast(F32).rearrange("p (m u) -> p m u", u=2),
+                v_bf[r].bitcast(F32).rearrange("p (m u) -> p m u", u=2),
                 turned[:].rearrange("p u m -> p m u"),
             )
 
-        def quantise_values(g):
-            v_codes[g] = placed.tile(
-                [P, 2 * P], U32, align_bytes=64, name="v_codes%d" % g, offset=last + 2048 + 1024 * g
-            )
-            nc.vector.quantize_mx(
-                out=v_codes[g][:].bitcast(FP8X4),
-                scales=v_scales[g][:],
-                in_=v_bf[g][:].rearrange("p a m t -> p (a m t)"),
-            )
+        def quantise_values(first, rounded):
+            feats = slice(first * P, first * P + rounded.shape[1] // PACK)
+            nc.vector.quantize_mx(out=v_codes[:, feats].bitcast(FP8X4), scales=v_scales[:, feats], in_=rounded)
 
         def product(out, r, h):
             cols = slice(h * P, (h + 1) * P)
-            feats = slice((r % 2) * P, (r % 2 + 1) * P)
+            feats = slice(r * P, (r + 1) * P)
             nc.tensor.matmul_mx(
                 out=out,
-                lhsT=v_codes[r // 2][:, feats].bitcast(FP8X4),
-                lhsT_scale=v_scales[r // 2][:, feats],
+                lhsT=v_codes[:, feats].bitcast(FP8X4),
+                lhsT_scale=v_scales[:, feats],
                 rhs=w_codes[:, cols].bitcast(FP8X4),
                 rhs_scale=w_scales[:, cols],
                 start=True,
@@ -248,25 +244,31 @@ def tile_attend_mixedbias_pl_kernel(
         for r in range(2, PACK):
             gather_values(r)
             turn_values(r)
+        v_codes = placed.tile([P, E], U32, align_bytes=64, offset=last + 2048)
         round_weights(0)
-        quantise_values(0)
+        quantise_values(0, v_bf_pair[:].rearrange("p a x -> p (a x)"))
         quantise_weights(0)
         round_weights(1)
-        quantise_values(1)
+        quantise_values(2, v_bf[2])
         quantise_weights(1)
+        quantise_values(3, v_bf[3])
 
         out_rows = out_0.rearrange("(p r) q -> p r q", r=PACK)
-        o_f32 = [sb.tile([P, PACK, P], F32, name="o_f32_%d" % h) for h in range(HALVES)]
+        o_f32 = [sb.tile([P, PACK, P], F32, align_bytes=256, name="o_f32_%d" % h) for h in range(HALVES)]
         o_bf = [sb.tile([P, P, PACK], BF16, align_bytes=64, name="o_bf%d" % h) for h in range(HALVES)]
-        o_codes = sb.tile([P, Q], U32, align_bytes=64)
-        o_scales = sb.tile([P, Q], U8, align_bytes=64)
+        o_codes = sb.tile([P, Q], U32, align_bytes=256)
+        o_scales = sb.tile([P, Q], U8, align_bytes=256)
+        results = [
+            [ps.tile([P, 2, P], F32, name="result%d%d" % (h, g), tag="bank%d" % (2 * h + g)) for g in range(2)]
+            for h in range(HALVES)
+        ]
+        for r in range(PACK):
+            for h in range(HALVES):
+                product(results[h][r // 2][:, r % 2, :], r, h)
+                if r % 2:
+                    nc.scalar.copy(o_f32[h][:, r - 1 : r + 1, :], results[h][r // 2][:])
         for h in range(HALVES):
             cols = slice(h * P, (h + 1) * P)
-            for g in range(2):
-                result = ps.tile([P, 2, P], F32, name="result%d%d" % (h, g), tag="bank%d" % (2 * h + g))
-                for a in range(2):
-                    product(result[:, a, :], 2 * g + a, h)
-                nc.scalar.copy(o_f32[h][:, 2 * g : 2 * g + 2, :], result[:])
             nc.sync.dma_start(out_rows[:, :, cols], o_f32[h][:])
             nc.vector.tensor_copy(o_bf[h][:], o_f32[h][:].rearrange("p r q -> p q r"))
             nc.vector.quantize_mx(

@@ -23,6 +23,8 @@ PACK = 4
 HALVES = Q // P
 BIAS_WINDOW = 704
 ROW_BYTES = 4 * T
+Q_RAW_AT = PACK * ROW_BYTES
+Q_BF_AT = Q_RAW_AT + 4 * PACK * Q
 
 
 def tile_attend_mixedbias_pl_kernel(
@@ -39,7 +41,7 @@ def tile_attend_mixedbias_pl_kernel(
         buckets = sb.tile([P, I // 16], U16)
         key_words = sb.tile([P, T], U16, align_bytes=256)
         key_scales = sb.tile([P, T], U8, align_bytes=256)
-        q_raw = sb.tile([P, PACK, Q], F32, align_bytes=256)
+        q_raw = placed.tile([P, PACK, Q], F32, align_bytes=256, offset=Q_RAW_AT)
         bias_rows = [sb.tile([P, BIAS_WINDOW], F32, align_bytes=256, name="bias_rows%d" % h) for h in range(HALVES)]
         gates = sb.tile([P, HALVES, 1], F32)
         sizes = sb.tile([P, PACK], F32)
@@ -47,14 +49,10 @@ def tile_attend_mixedbias_pl_kernel(
             placed.tile([P, T], F32, align_bytes=256, name="v_raw%d" % r, offset=r * ROW_BYTES) for r in range(PACK)
         ]
         ident = sb.tile([P, P], F32)
-        warm = sb.tile([P, 1], F32)
-        warm_out = sb.tile([P, 1], F32)
 
         nc.gpsimd.memset(key_scales[:].bitcast(I32), 0)
         for h in range(HALVES):
             nc.vector.memset(bias_rows[h][:, U:], 0.0)
-        nc.vector.memset(warm[:], 0.0)
-        nc.scalar.activation(warm_out[:], warm[:], ACT.Exp)
         make_identity(nc, ident[:])
 
         nc.sync.dma_start(buckets[:], offs2)
@@ -76,26 +74,35 @@ def tile_attend_mixedbias_pl_kernel(
         for r in range(1, PACK):
             nc.sync.dma_start(v_raw[r][:], vals_dealt[r])
 
-        slot_bias = [sb.tile([P, I], F32, name="slot_bias%d" % h) for h in range(HALVES)]
-        k_words = sb.tile([P, I], U16, align_bytes=64)
+        slot_bias = [sb.tile([P, I], F32, name="slot_bias0"), None]
         k_scales = sb.tile([P, I], U8, align_bytes=64)
-        q_bf = [sb.tile([P, P, PACK], BF16, align_bytes=64, name="q_bf%d" % h) for h in range(HALVES)]
+        q_bf = [
+            placed.tile([P, P, PACK], BF16, align_bytes=64, name="q_bf0", offset=Q_BF_AT),
+            sb.tile([P, P, PACK], BF16, align_bytes=64, name="q_bf1"),
+        ]
         q_codes = sb.tile([P, Q], U32, align_bytes=64)
         q_scales = sb.tile([P, Q], U8, align_bytes=64)
         scores = [ps.tile([P, I], F32, name="scores%d" % h, tag="bank%d" % h) for h in range(HALVES)]
 
         nc.vector.tensor_copy(slot_bias[0][:], bias_rows[0][:].indirect(buckets[:]))
         nc.vector.tensor_copy(k_scales[:], key_scales[:].indirect(slots[:]))
-        nc.vector.tensor_copy(k_words[:], key_words[:].indirect(slots[:]))
         for h in range(HALVES):
             nc.scalar.copy(q_bf[h][:], q_raw[:, :, h * P : (h + 1) * P].rearrange("p j q -> p q j"))
-        for h in range(HALVES):
+
+        def quantise_queries(h):
             cols = slice(h * P, (h + 1) * P)
             nc.vector.quantize_mx(
                 out=q_codes[:, cols].bitcast(FP8X4),
                 scales=q_scales[:, cols],
                 in_=q_bf[h][:].rearrange("p q j -> p (q j)"),
             )
+
+        quantise_queries(0)
+        k_words = placed.tile([P, I], U16, align_bytes=64, offset=Q_BF_AT)
+        nc.vector.tensor_copy(k_words[:], key_words[:].indirect(slots[:]))
+        quantise_queries(1)
+        for h in range(HALVES):
+            cols = slice(h * P, (h + 1) * P)
             nc.tensor.matmul_mx(
                 out=scores[h][:],
                 lhsT=q_codes[:, cols].bitcast(FP8X4),
@@ -105,6 +112,7 @@ def tile_attend_mixedbias_pl_kernel(
                 start=True,
                 stop=True,
             )
+        slot_bias[1] = placed.tile([P, I], F32, align_bytes=64, name="slot_bias1", offset=Q_RAW_AT)
         nc.vector.tensor_copy(slot_bias[1][:], bias_rows[1][:].indirect(buckets[:]))
 
         rest = sb.tile([P, HALVES, 1], F32)
@@ -270,7 +278,12 @@ def tile_attend_mixedbias_pl_kernel(
         for h in range(HALVES):
             cols = slice(h * P, (h + 1) * P)
             nc.sync.dma_start(out_rows[:, :, cols], o_f32[h][:])
-            nc.vector.tensor_copy(o_bf[h][:], o_f32[h][:].rearrange("p r q -> p q r"))
+            nc.vector.tensor_copy(
+                o_bf[h][:].rearrange("p (c i) r -> p c r i", i=4),
+                o_f32[h][:].rearrange("p r (c i) -> p c r i", i=4),
+            )
+        for h in range(HALVES):
+            cols = slice(h * P, (h + 1) * P)
             nc.vector.quantize_mx(
                 out=o_codes[:, cols].bitcast(FP8X4),
                 scales=o_scales[:, cols],

@@ -22,9 +22,9 @@ P = 128
 PACK = 4
 HALVES = Q // P
 BIAS_WINDOW = 704
+ZERO_SPLIT = 1280
 ROW_BYTES = 4 * T
 Q_RAW_AT = PACK * ROW_BYTES
-Q_BF_AT = Q_RAW_AT + 4 * PACK * Q
 
 
 def tile_attend_mixedbias_pl_kernel(
@@ -41,7 +41,10 @@ def tile_attend_mixedbias_pl_kernel(
         buckets = sb.tile([P, I // 16], U16)
         key_words = sb.tile([P, T], U16, align_bytes=256)
         key_scales = sb.tile([P, T], U8, align_bytes=256)
-        q_raw = placed.tile([P, PACK, Q], F32, align_bytes=256, offset=Q_RAW_AT)
+        q_raw = [
+            placed.tile([P, PACK, P], F32, align_bytes=256, name="q_raw0", offset=Q_RAW_AT),
+            sb.tile([P, PACK, P], F32, align_bytes=256, name="q_raw1"),
+        ]
         bias_rows = [sb.tile([P, BIAS_WINDOW], F32, align_bytes=256, name="bias_rows%d" % h) for h in range(HALVES)]
         gates = sb.tile([P, HALVES, 1], F32)
         sizes = sb.tile([P, PACK], F32)
@@ -50,7 +53,8 @@ def tile_attend_mixedbias_pl_kernel(
         ]
         ident = sb.tile([P, P], F32)
 
-        nc.gpsimd.memset(key_scales[:].bitcast(I32), 0)
+        nc.vector.memset(key_scales[:, :ZERO_SPLIT].bitcast(I32), 0)
+        nc.gpsimd.memset(key_scales[:, ZERO_SPLIT:].bitcast(I32), 0)
         for h in range(HALVES):
             nc.vector.memset(bias_rows[h][:, U:], 0.0)
         make_identity(nc, ident[:])
@@ -59,13 +63,16 @@ def tile_attend_mixedbias_pl_kernel(
         nc.sync.dma_start(bias_rows[0][:, :U], bias[:P, :])
         nc.sync.dma_start(slots[:], offs)
         for c in range(4):
-            nc.sync.dma_start(
+            queue = nc.sync if c < 2 else nc.scalar
+            queue.dma_start(
                 key_scales[c:P:32, :].bitcast(I32),
                 keys_scales[0, c:16:4, :].bitcast(I32),
             )
-        nc.sync.dma_start(q_raw[:], query.rearrange("(p j) q -> p j q", j=PACK))
+        q_dealt = query.rearrange("(p j) q -> p j q", j=PACK)
         nc.sync.dma_start(key_words[:].bitcast(I32), keys_words[0].bitcast(I32))
+        nc.sync.dma_start(q_raw[0][:], q_dealt[:, :, :P])
         nc.sync.dma_start(bias_rows[1][:, :U], bias[P:, :])
+        nc.sync.dma_start(q_raw[1][:], q_dealt[:, :, P:])
         vals_dealt = vals.rearrange("(p r) t -> r p t", r=PACK)
         nc.sync.dma_start(v_raw[0][:], vals_dealt[0])
         with nc.allow_non_contiguous_dma(reason="one gate for each partition and half"):
@@ -76,33 +83,25 @@ def tile_attend_mixedbias_pl_kernel(
 
         slot_bias = [sb.tile([P, I], F32, name="slot_bias0"), None]
         k_scales = sb.tile([P, I], U8, align_bytes=64)
-        q_bf = [
-            placed.tile([P, P, PACK], BF16, align_bytes=64, name="q_bf0", offset=Q_BF_AT),
-            sb.tile([P, P, PACK], BF16, align_bytes=64, name="q_bf1"),
-        ]
+        q_bf = [sb.tile([P, P, PACK], BF16, align_bytes=64, name="q_bf%d" % h) for h in range(HALVES)]
         q_codes = sb.tile([P, Q], U32, align_bytes=64)
         q_scales = sb.tile([P, Q], U8, align_bytes=64)
         scores = [ps.tile([P, I], F32, name="scores%d" % h, tag="bank%d" % h) for h in range(HALVES)]
 
         nc.vector.tensor_copy(slot_bias[0][:], bias_rows[0][:].indirect(buckets[:]))
         nc.vector.tensor_copy(k_scales[:], key_scales[:].indirect(slots[:]))
+        k_words = sb.tile([P, I], U16, align_bytes=64)
+        nc.vector.tensor_copy(k_words[:], key_words[:].indirect(slots[:]))
         for h in range(HALVES):
-            nc.scalar.copy(q_bf[h][:], q_raw[:, :, h * P : (h + 1) * P].rearrange("p j q -> p q j"))
+            nc.scalar.copy(q_bf[h][:], q_raw[h][:].rearrange("p j q -> p q j"))
 
-        def quantise_queries(h):
+        def score(h):
             cols = slice(h * P, (h + 1) * P)
             nc.vector.quantize_mx(
                 out=q_codes[:, cols].bitcast(FP8X4),
                 scales=q_scales[:, cols],
                 in_=q_bf[h][:].rearrange("p q j -> p (q j)"),
             )
-
-        quantise_queries(0)
-        k_words = placed.tile([P, I], U16, align_bytes=64, offset=Q_BF_AT)
-        nc.vector.tensor_copy(k_words[:], key_words[:].indirect(slots[:]))
-        quantise_queries(1)
-        for h in range(HALVES):
-            cols = slice(h * P, (h + 1) * P)
             nc.tensor.matmul_mx(
                 out=scores[h][:],
                 lhsT=q_codes[:, cols].bitcast(FP8X4),
@@ -112,8 +111,11 @@ def tile_attend_mixedbias_pl_kernel(
                 start=True,
                 stop=True,
             )
-        slot_bias[1] = placed.tile([P, I], F32, align_bytes=64, name="slot_bias1", offset=Q_RAW_AT)
+
+        score(0)
+        slot_bias[1] = placed.tile([P, I], F32, align_bytes=256, name="slot_bias1", offset=Q_RAW_AT)
         nc.vector.tensor_copy(slot_bias[1][:], bias_rows[1][:].indirect(buckets[:]))
+        score(1)
 
         rest = sb.tile([P, HALVES, 1], F32)
         nc.gpsimd.tensor_scalar(rest[:], gates[:], -1.0, 1.0, ALU.mult, ALU.add)
@@ -129,14 +131,14 @@ def tile_attend_mixedbias_pl_kernel(
         ]
         v_scales = sb.tile([P, E], U8, align_bytes=64)
         exps = [sb.tile([P, 2, PACK, P], F32, name="exps%d" % h) for h in range(HALVES)]
-        sums = sb.tile([P, 2, HALVES], F32)
-        inv = sb.tile([P, 2, HALVES], F32)
+        sums = sb.tile([P, 2 * HALVES], F32)
+        inv = sb.tile([P, 2 * HALVES], F32)
         biased = [sb.tile([P, I], F32, name="biased%d" % h) for h in range(HALVES)]
         neg_max_a = [sb.tile([P, 1], F32, name="neg_max_a%d" % h) for h in range(HALVES)]
         neg_max_s = [sb.tile([P, 1], F32, name="neg_max_s%d" % h) for h in range(HALVES)]
         parts = [sb.tile([P, 2, PACK, P], F32, name="parts%d" % h) for h in range(HALVES)]
         coef = [sb.tile([P, 2], F32, name="coef%d" % h) for h in range(HALVES)]
-        w_turned = [ps.tile([P, PACK, P], F32, name="w_turned%d" % h) for h in range(HALVES)]
+        w_turned = [ps.tile([P, PACK, P], F32, name="w_turned%d" % h, tag="w_turned%d" % h) for h in range(HALVES)]
 
         def plain_max(h):
             nc.vector.tensor_reduce(neg_max_a[h][:], scores[h][:], AX.X, ALU.max, negate=True)
@@ -148,7 +150,7 @@ def tile_attend_mixedbias_pl_kernel(
                 scores[h][:].rearrange("p (s t) -> p t s", t=PACK),
                 ACT.Exp,
                 bias=neg_max_a[h][:],
-                accum_out=sums[:, 1, h : h + 1],
+                accum_out=sums[:, h : h + 1],
             )
 
         def biased_exp(h):
@@ -158,11 +160,12 @@ def tile_attend_mixedbias_pl_kernel(
                 biased[h][:].rearrange("p (s t) -> p s t", t=PACK),
                 ACT.Exp,
                 bias=neg_max_s[h][:],
-                accum_out=sums[:, 0, h : h + 1],
+                accum_out=sums[:, HALVES + h : HALVES + h + 1],
             )
 
         def scale_part(h, k):
-            nc.scalar.activation(coef[h][:, k : k + 1], inv[:, k, h : h + 1], ACT.Copy, scale=shares[k][:, h, :])
+            at = (1 - k) * HALVES + h
+            nc.scalar.activation(coef[h][:, k : k + 1], inv[:, at : at + 1], ACT.Copy, scale=shares[k][:, h, :])
             nc.scalar.activation(parts[h][:, k], exps[h][:, k], ACT.Copy, scale=coef[h][:, k : k + 1])
 
         def turn_part(h, k):
@@ -230,25 +233,23 @@ def tile_attend_mixedbias_pl_kernel(
         for h in range(HALVES):
             plain_max(h)
             add_bias(h)
-        nc.vector.reciprocal(inv[:, 1, 0:1], sums[:, 1, 0:1])
+        nc.vector.reciprocal(inv[:, 0:1], sums[:, 0:1])
         for h in range(HALVES):
             biased_exp(h)
-        nc.vector.tensor_scalar(
-            parts[0][:, 1], exps[0][:, 1], inv[:, 1, 0:1], shares[1][:, 0, :], ALU.mult, ALU.mult
-        )
+        nc.vector.tensor_scalar(parts[0][:, 1], exps[0][:, 1], inv[:, 0:1], shares[1][:, 0, :], ALU.mult, ALU.mult)
         turn_part(0, 1)
-        nc.vector.reciprocal(inv[:, 1, 1:2], sums[:, 1, 1:2])
-        scale_part(1, 1)
-        gather_values(0)
-        nc.vector.reciprocal(inv[:, 0, :], sums[:, 0, :])
+        nc.vector.reciprocal(inv[:, 1:3], sums[:, 1:3])
         scale_part(0, 0)
-        turn_values(0)
-        turn_part(1, 1)
         turn_part(0, 0)
-        gather_values(1)
+        scale_part(1, 1)
+        turn_part(1, 1)
+        gather_values(0)
+        nc.vector.reciprocal(inv[:, 3:4], sums[:, 3:4])
         scale_part(1, 0)
-        turn_values(1)
+        turn_values(0)
         turn_part(1, 0)
+        gather_values(1)
+        turn_values(1)
         for r in range(2, PACK):
             gather_values(r)
             turn_values(r)
@@ -266,15 +267,20 @@ def tile_attend_mixedbias_pl_kernel(
         o_bf = [sb.tile([P, P, PACK], BF16, align_bytes=64, name="o_bf%d" % h) for h in range(HALVES)]
         o_codes = sb.tile([P, Q], U32, align_bytes=256)
         o_scales = sb.tile([P, Q], U8, align_bytes=256)
-        results = [
-            [ps.tile([P, 2, P], F32, name="result%d%d" % (h, g), tag="bank%d" % (2 * h + g)) for g in range(2)]
-            for h in range(HALVES)
-        ]
+        groups = (((0, 1), (2,), (3,)), ((0, 1), (2, 3)))
+        banks = (("bank0", "bank1", "w_turned0"), ("bank2", "bank3"))
+        results = {}
+        for h in range(HALVES):
+            for rows, bank in zip(groups[h], banks[h]):
+                held = ps.tile([P, len(rows), P], F32, name="result%d%d" % (h, rows[0]), tag=bank)
+                for r in rows:
+                    results[h, r] = (held, rows)
         for r in range(PACK):
             for h in range(HALVES):
-                product(results[h][r // 2][:, r % 2, :], r, h)
-                if r % 2:
-                    nc.scalar.copy(o_f32[h][:, r - 1 : r + 1, :], results[h][r // 2][:])
+                held, rows = results[h, r]
+                product(held[:, r - rows[0], :], r, h)
+                if r == rows[-1]:
+                    nc.scalar.copy(o_f32[h][:, rows[0] : r + 1, :], held[:])
         for h in range(HALVES):
             cols = slice(h * P, (h + 1) * P)
             nc.sync.dma_start(out_rows[:, :, cols], o_f32[h][:])
@@ -289,9 +295,7 @@ def tile_attend_mixedbias_pl_kernel(
                 scales=o_scales[:, cols],
                 in_=o_bf[h][:].rearrange("p q r -> p (q r)"),
             )
-            nc.sync.dma_start(
-                out_1[0].rearrange("p q r -> p (q r)").bitcast(I32)[:, cols], o_codes[:, cols].bitcast(I32)
-            )
+        nc.sync.dma_start(out_1[0].rearrange("p q r -> p (q r)").bitcast(I32), o_codes[:].bitcast(I32))
         for c in range(4):
             queue = nc.sync if c < 2 else nc.scalar
             queue.dma_start(

@@ -21,10 +21,13 @@ AX = mybir.AxisListType
 P = 128
 PACK = 4
 HALVES = Q // P
-BIAS_WINDOW = 704
+BIAS_WINDOW = U + 8
 ZERO_SPLIT = 1280
 ROW_BYTES = 4 * T
 Q_RAW_AT = PACK * ROW_BYTES
+EXP_AT = Q_RAW_AT + 8 * I
+LIST_COLS = I // 16
+LAST_SPLIT = 20
 
 
 def tile_attend_mixedbias_pl_kernel(
@@ -35,19 +38,16 @@ def tile_attend_mixedbias_pl_kernel(
         sb = ctx.enter_context(tc.tile_pool(name="sb", bufs=1))
         placed = ctx.enter_context(tc.tile_pool(name="placed", bufs=1))
         ps = ctx.enter_context(tc.psum_pool(name="ps", bufs=1))
-        ps_turn = ctx.enter_context(tc.psum_pool(name="ps_turn", bufs=2))
 
         slots = sb.tile([P, I // 16], U16)
         buckets = sb.tile([P, I // 16], U16)
         key_words = sb.tile([P, T], U16, align_bytes=256)
         key_scales = sb.tile([P, T], U8, align_bytes=256)
         q_raw = [
-            placed.tile([P, PACK, P], F32, align_bytes=256, name="q_raw0", offset=Q_RAW_AT),
-            sb.tile([P, PACK, P], F32, align_bytes=256, name="q_raw1"),
+            placed.tile([P, PACK, P], F32, align_bytes=256, name="q_raw0", offset=Q_RAW_AT + 4 * I),
+            placed.tile([P, PACK, P], F32, align_bytes=256, name="q_raw1", offset=Q_RAW_AT),
         ]
         bias_rows = [sb.tile([P, BIAS_WINDOW], F32, align_bytes=256, name="bias_rows%d" % h) for h in range(HALVES)]
-        gates = sb.tile([P, HALVES, 1], F32)
-        sizes = sb.tile([P, PACK], F32)
         v_raw = [
             placed.tile([P, T], F32, align_bytes=256, name="v_raw%d" % r, offset=r * ROW_BYTES) for r in range(PACK)
         ]
@@ -59,41 +59,40 @@ def tile_attend_mixedbias_pl_kernel(
             nc.vector.memset(bias_rows[h][:, U:], 0.0)
         make_identity(nc, ident[:])
 
-        nc.sync.dma_start(buckets[:], offs2)
-        nc.sync.dma_start(bias_rows[0][:, :U], bias[:P, :])
+        q_dealt = query.rearrange("(p j) q -> p j q", j=PACK)
         nc.sync.dma_start(slots[:], offs)
+        nc.sync.dma_start(q_raw[0][:], q_dealt[:, :, :P])
         for c in range(4):
             queue = nc.sync if c < 2 else nc.scalar
             queue.dma_start(
                 key_scales[c:P:32, :].bitcast(I32),
                 keys_scales[0, c:16:4, :].bitcast(I32),
             )
-        q_dealt = query.rearrange("(p j) q -> p j q", j=PACK)
         nc.sync.dma_start(key_words[:].bitcast(I32), keys_words[0].bitcast(I32))
-        nc.sync.dma_start(q_raw[0][:], q_dealt[:, :, :P])
-        nc.sync.dma_start(bias_rows[1][:, :U], bias[P:, :])
+        nc.sync.dma_start(buckets[:], offs2)
+        nc.sync.dma_start(bias_rows[0][:, :U], bias[:P, :])
         nc.sync.dma_start(q_raw[1][:], q_dealt[:, :, P:])
+        nc.sync.dma_start(bias_rows[1][:, :U], bias[P:, :])
         vals_dealt = vals.rearrange("(p r) t -> r p t", r=PACK)
-        nc.sync.dma_start(v_raw[0][:], vals_dealt[0])
-        with nc.allow_non_contiguous_dma(reason="one gate for each partition and half"):
-            nc.sync.dma_start(gates[:], gate.rearrange("(h p) o -> p h o", p=P))
-        nc.sync.dma_start(sizes[:], size.rearrange("o (p t) -> p (o t)", t=PACK))
-        for r in range(1, PACK):
+        for r in range(PACK):
             nc.sync.dma_start(v_raw[r][:], vals_dealt[r])
 
-        slot_bias = [sb.tile([P, I], F32, name="slot_bias0"), None]
+        slot_bias = [sb.tile([P, I], F32, name="slot_bias%d" % h) for h in range(HALVES)]
         k_scales = sb.tile([P, I], U8, align_bytes=64)
         q_bf = [sb.tile([P, P, PACK], BF16, align_bytes=64, name="q_bf%d" % h) for h in range(HALVES)]
         q_codes = sb.tile([P, Q], U32, align_bytes=64)
         q_scales = sb.tile([P, Q], U8, align_bytes=64)
         scores = [ps.tile([P, I], F32, name="scores%d" % h, tag="bank%d" % h) for h in range(HALVES)]
 
-        nc.vector.tensor_copy(slot_bias[0][:], bias_rows[0][:].indirect(buckets[:]))
+        nc.scalar.copy(q_bf[0][:], q_raw[0][:].rearrange("p j q -> p q j"))
+        gates = placed.tile([P, HALVES, 1], F32, offset=Q_RAW_AT + 4 * I)
+        sizes = placed.tile([P, PACK], F32, offset=Q_RAW_AT + 4 * I + 32)
+        with nc.allow_non_contiguous_dma(reason="one gate for each partition and half"):
+            nc.scalar.dma_start(gates[:], gate.rearrange("(h p) o -> p h o", p=P))
+        nc.scalar.dma_start(sizes[:], size.rearrange("o (p t) -> p (o t)", t=PACK))
         nc.vector.tensor_copy(k_scales[:], key_scales[:].indirect(slots[:]))
         k_words = sb.tile([P, I], U16, align_bytes=64)
         nc.vector.tensor_copy(k_words[:], key_words[:].indirect(slots[:]))
-        for h in range(HALVES):
-            nc.scalar.copy(q_bf[h][:], q_raw[h][:].rearrange("p j q -> p q j"))
 
         def score(h):
             cols = slice(h * P, (h + 1) * P)
@@ -113,9 +112,10 @@ def tile_attend_mixedbias_pl_kernel(
             )
 
         score(0)
-        slot_bias[1] = placed.tile([P, I], F32, align_bytes=256, name="slot_bias1", offset=Q_RAW_AT)
-        nc.vector.tensor_copy(slot_bias[1][:], bias_rows[1][:].indirect(buckets[:]))
+        nc.vector.tensor_copy(q_bf[1][:], q_raw[1][:].rearrange("p j q -> p q j"))
         score(1)
+        for h in range(HALVES):
+            nc.scalar.activation(slot_bias[h][:], bias_rows[h][:].indirect(buckets[:]), ACT.Copy)
 
         rest = sb.tile([P, HALVES, 1], F32)
         nc.gpsimd.tensor_scalar(rest[:], gates[:], -1.0, 1.0, ALU.mult, ALU.add)
@@ -123,18 +123,27 @@ def tile_attend_mixedbias_pl_kernel(
 
         last = (PACK - 1) * ROW_BYTES
         w_bf = [None] * HALVES
-        w_codes = sb.tile([P, Q], U32, align_bytes=64)
+        w_codes = placed.tile([P, Q], U32, align_bytes=64, offset=last + 1024)
         w_scales = sb.tile([P, Q], U8, align_bytes=64)
-        v_bf_pair = sb.tile([P, 2, P * PACK], BF16, align_bytes=64)
-        v_bf = [v_bf_pair[:, 0, :], v_bf_pair[:, 1, :]] + [
-            sb.tile([P, P * PACK], BF16, align_bytes=64, name="v_bf%d" % r)[:] for r in range(2, PACK)
+        v_bf = [
+            placed.tile([P, I], BF16, align_bytes=64, name="v_bf0", offset=ROW_BYTES)[:],
+            placed.tile([P, I], BF16, align_bytes=64, name="v_bf1", offset=last + 2048)[:],
+            placed.tile([P, I], BF16, align_bytes=64, name="v_bf2", offset=last + 3072)[:],
+            sb.tile([P, I], BF16, align_bytes=64, name="v_bf3")[:],
         ]
+        v_codes = placed.tile([P, E], U32, align_bytes=64, offset=last + 4096)
         v_scales = sb.tile([P, E], U8, align_bytes=64)
-        exps = [sb.tile([P, 2, PACK, P], F32, name="exps%d" % h) for h in range(HALVES)]
+        exps = [
+            placed.tile([P, 2, PACK, P], F32, name="exps0", offset=EXP_AT),
+            sb.tile([P, 2, PACK, P], F32, name="exps1"),
+        ]
         sums = sb.tile([P, 2 * HALVES], F32)
         inv = sb.tile([P, 2 * HALVES], F32)
         biased = [sb.tile([P, I], F32, name="biased%d" % h) for h in range(HALVES)]
-        neg_max_a = [sb.tile([P, 1], F32, name="neg_max_a%d" % h) for h in range(HALVES)]
+        neg_max_a = [
+            placed.tile([P, 1], F32, name="neg_max_a0", offset=Q_RAW_AT),
+            sb.tile([P, 1], F32, name="neg_max_a1"),
+        ]
         neg_max_s = [sb.tile([P, 1], F32, name="neg_max_s%d" % h) for h in range(HALVES)]
         parts = [sb.tile([P, 2, PACK, P], F32, name="parts%d" % h) for h in range(HALVES)]
         coef = [sb.tile([P, 2], F32, name="coef%d" % h) for h in range(HALVES)]
@@ -168,6 +177,12 @@ def tile_attend_mixedbias_pl_kernel(
             nc.scalar.activation(coef[h][:, k : k + 1], inv[:, at : at + 1], ACT.Copy, scale=shares[k][:, h, :])
             nc.scalar.activation(parts[h][:, k], exps[h][:, k], ACT.Copy, scale=coef[h][:, k : k + 1])
 
+        def scale_on_vector(h, k):
+            at = (1 - k) * HALVES + h
+            nc.vector.tensor_scalar(
+                parts[h][:, k], exps[h][:, k], inv[:, at : at + 1], shares[k][:, h, :], ALU.mult, ALU.mult
+            )
+
         def turn_part(h, k):
             for t in range(PACK):
                 nc.tensor.matmul(
@@ -181,7 +196,7 @@ def tile_attend_mixedbias_pl_kernel(
 
         def round_weights(h):
             w_bf[h] = placed.tile(
-                [P, P, PACK], BF16, align_bytes=64, name="w_bf%d" % h, offset=last + 1024 * h
+                [P, P, PACK], BF16, align_bytes=64, name="w_bf%d" % h, offset=(2 + h) * ROW_BYTES
             )
             nc.vector.tensor_tensor(
                 w_bf[h][:],
@@ -198,16 +213,24 @@ def tile_attend_mixedbias_pl_kernel(
                 in_=w_bf[h][:].rearrange("p q t -> p (q t)"),
             )
 
-        listed = [sb.tile([P, I], BF16, name="listed%d" % r) for r in range(PACK)]
+        listed = [
+            sb.tile([P, I], BF16, name="listed0"),
+            placed.tile([P, I], BF16, name="listed1", offset=EXP_AT),
+            sb.tile([P, I], BF16, name="listed2"),
+            sb.tile([P, I], BF16, name="listed3"),
+        ]
 
         def gather_values(r):
             nc.vector.tensor_copy(listed[r][:], v_raw[r][:].indirect(slots[:]))
 
         def turn_values(r):
             pairs = listed[r][:].bitcast(F32)
-            turned = ps_turn.tile([P, 2, P], F32, name="turned")
+            turned = ps.tile([P, 2, P], F32, name="turned%d" % r, tag=("turned0", "turned1", "bank2", "bank3")[r])
             for u in range(2):
                 nc.tensor.transpose(turned[:, u, :], pairs[:, u::2], ident[:])
+            return turned
+
+        def copy_values(r, turned):
             nc.scalar.copy(
                 v_bf[r].bitcast(F32).rearrange("p (m u) -> p m u", u=2),
                 turned[:].rearrange("p u m -> p m u"),
@@ -236,28 +259,34 @@ def tile_attend_mixedbias_pl_kernel(
         nc.vector.reciprocal(inv[:, 0:1], sums[:, 0:1])
         for h in range(HALVES):
             biased_exp(h)
-        nc.vector.tensor_scalar(parts[0][:, 1], exps[0][:, 1], inv[:, 0:1], shares[1][:, 0, :], ALU.mult, ALU.mult)
-        turn_part(0, 1)
-        nc.vector.reciprocal(inv[:, 1:3], sums[:, 1:3])
+        nc.vector.reciprocal(inv[:, 1:2], sums[:, 1:2])
+        for h in range(HALVES):
+            scale_on_vector(h, 1)
+            turn_part(h, 1)
+        nc.vector.reciprocal(inv[:, 2:3], sums[:, 2:3])
         scale_part(0, 0)
         turn_part(0, 0)
-        scale_part(1, 1)
-        turn_part(1, 1)
         gather_values(0)
         nc.vector.reciprocal(inv[:, 3:4], sums[:, 3:4])
-        scale_part(1, 0)
-        turn_values(0)
+        scale_on_vector(1, 0)
         turn_part(1, 0)
-        gather_values(1)
-        turn_values(1)
-        for r in range(2, PACK):
-            gather_values(r)
-            turn_values(r)
-        v_codes = placed.tile([P, E], U32, align_bytes=64, offset=last + 2048)
+        turned = [turn_values(0)]
+        nc.scalar.activation(listed[1][:], v_raw[1][:].indirect(slots[:]), ACT.Copy)
+        turned.append(turn_values(1))
+        gather_values(2)
+        turned.append(turn_values(2))
+        copy_values(0, turned[0])
         round_weights(0)
-        quantise_values(0, v_bf_pair[:].rearrange("p a x -> p (a x)"))
+        shared = 16 * LAST_SPLIT
+        nc.vector.tensor_copy(listed[3][:, :shared], v_raw[3][:].indirect(slots[:, :LAST_SPLIT]))
+        nc.scalar.activation(listed[3][:, shared:], v_raw[3][:].indirect(slots[:, LAST_SPLIT:]), ACT.Copy)
+        turned.append(turn_values(3))
+        for r in range(1, PACK):
+            copy_values(r, turned[r])
         quantise_weights(0)
+        quantise_values(0, v_bf[0])
         round_weights(1)
+        quantise_values(1, v_bf[1])
         quantise_values(2, v_bf[2])
         quantise_weights(1)
         quantise_values(3, v_bf[3])

@@ -22,12 +22,15 @@ P = 128
 PACK = 4
 HALVES = Q // P
 BIAS_WINDOW = U + 8
-ZERO_SPLIT = 1280
+SCALE_ROWS = 16
+SCALES_AT = P - SCALE_ROWS
 ROW_BYTES = 4 * T
 Q_RAW_AT = PACK * ROW_BYTES
 EXP_AT = Q_RAW_AT + 8 * I
-LIST_COLS = I // 16
-LAST_SPLIT = 20
+Q_BF_AT = EXP_AT + 8 * I
+PLAIN_AT = Q_BF_AT + 2 * I
+NEG_AT = PLAIN_AT + 8 * I
+LAST_SPLIT = 16
 
 
 def tile_attend_mixedbias_pl_kernel(
@@ -53,54 +56,60 @@ def tile_attend_mixedbias_pl_kernel(
         ]
         ident = sb.tile([P, P], F32)
 
-        nc.vector.memset(key_scales[:, :ZERO_SPLIT].bitcast(I32), 0)
-        nc.gpsimd.memset(key_scales[:, ZERO_SPLIT:].bitcast(I32), 0)
+        listed_scales = sb.tile([P, I], U8, align_bytes=256)
+        k_scales = sb.tile([P, I], U8, align_bytes=256)
+        gates = sb.tile([P, HALVES, 1], F32)
+        sizes = sb.tile([P, PACK], F32)
+        nc.vector.memset(key_scales[:SCALES_AT, :].bitcast(I32), 0)
+        nc.gpsimd.memset(k_scales[:].bitcast(I32), 0)
         for h in range(HALVES):
-            nc.vector.memset(bias_rows[h][:, U:], 0.0)
+            nc.gpsimd.memset(bias_rows[h][:, U:], 0.0)
         make_identity(nc, ident[:])
 
         q_dealt = query.rearrange("(p j) q -> p j q", j=PACK)
         nc.sync.dma_start(slots[:], offs)
+        nc.sync.dma_start(key_scales[SCALES_AT:, :].bitcast(I32), keys_scales[0].bitcast(I32))
         nc.sync.dma_start(q_raw[0][:], q_dealt[:, :, :P])
-        for c in range(4):
-            queue = nc.sync if c < 2 else nc.scalar
-            queue.dma_start(
-                key_scales[c:P:32, :].bitcast(I32),
-                keys_scales[0, c:16:4, :].bitcast(I32),
-            )
         nc.sync.dma_start(key_words[:].bitcast(I32), keys_words[0].bitcast(I32))
         nc.sync.dma_start(buckets[:], offs2)
+        with nc.allow_non_contiguous_dma(reason="one gate for each partition and half"):
+            nc.sync.dma_start(gates[:], gate.rearrange("(h p) o -> p h o", p=P))
         nc.sync.dma_start(bias_rows[0][:, :U], bias[:P, :])
         nc.sync.dma_start(q_raw[1][:], q_dealt[:, :, P:])
         nc.sync.dma_start(bias_rows[1][:, :U], bias[P:, :])
+        nc.vector.tensor_copy(listed_scales[:], key_scales[:].indirect(slots[:]))
+        for c in range(4):
+            nc.sync.dma_start(
+                k_scales[c:P:32, :].bitcast(I32),
+                listed_scales[SCALES_AT + c : P : 4, :].bitcast(I32),
+            )
         vals_dealt = vals.rearrange("(p r) t -> r p t", r=PACK)
-        for r in range(PACK):
+        nc.sync.dma_start(v_raw[0][:], vals_dealt[0])
+        nc.sync.dma_start(sizes[:], size.rearrange("o (p t) -> p (o t)", t=PACK))
+        for r in range(1, PACK):
             nc.sync.dma_start(v_raw[r][:], vals_dealt[r])
 
         slot_bias = [sb.tile([P, I], F32, name="slot_bias%d" % h) for h in range(HALVES)]
-        k_scales = sb.tile([P, I], U8, align_bytes=64)
-        q_bf = [sb.tile([P, P, PACK], BF16, align_bytes=64, name="q_bf%d" % h) for h in range(HALVES)]
+        q_bf = [
+            placed.tile([P, P, PACK], BF16, align_bytes=64, name="q_bf0", offset=Q_BF_AT),
+            sb.tile([P, P, PACK], BF16, align_bytes=64, name="q_bf1"),
+        ]
         q_codes = sb.tile([P, Q], U32, align_bytes=64)
         q_scales = sb.tile([P, Q], U8, align_bytes=64)
         scores = [ps.tile([P, I], F32, name="scores%d" % h, tag="bank%d" % h) for h in range(HALVES)]
 
         nc.scalar.copy(q_bf[0][:], q_raw[0][:].rearrange("p j q -> p q j"))
-        gates = placed.tile([P, HALVES, 1], F32, offset=Q_RAW_AT + 4 * I)
-        sizes = placed.tile([P, PACK], F32, offset=Q_RAW_AT + 4 * I + 32)
-        with nc.allow_non_contiguous_dma(reason="one gate for each partition and half"):
-            nc.scalar.dma_start(gates[:], gate.rearrange("(h p) o -> p h o", p=P))
-        nc.scalar.dma_start(sizes[:], size.rearrange("o (p t) -> p (o t)", t=PACK))
-        nc.vector.tensor_copy(k_scales[:], key_scales[:].indirect(slots[:]))
-        k_words = sb.tile([P, I], U16, align_bytes=64)
-        nc.vector.tensor_copy(k_words[:], key_words[:].indirect(slots[:]))
 
-        def score(h):
+        def quantise_queries(h):
             cols = slice(h * P, (h + 1) * P)
             nc.vector.quantize_mx(
                 out=q_codes[:, cols].bitcast(FP8X4),
                 scales=q_scales[:, cols],
                 in_=q_bf[h][:].rearrange("p q j -> p (q j)"),
             )
+
+        def score(h):
+            cols = slice(h * P, (h + 1) * P)
             nc.tensor.matmul_mx(
                 out=scores[h][:],
                 lhsT=q_codes[:, cols].bitcast(FP8X4),
@@ -111,8 +120,12 @@ def tile_attend_mixedbias_pl_kernel(
                 stop=True,
             )
 
+        quantise_queries(0)
+        k_words = placed.tile([P, I], U16, align_bytes=64, offset=Q_BF_AT)
+        nc.vector.tensor_copy(k_words[:], key_words[:].indirect(slots[:]))
         score(0)
         nc.vector.tensor_copy(q_bf[1][:], q_raw[1][:].rearrange("p j q -> p q j"))
+        quantise_queries(1)
         score(1)
         for h in range(HALVES):
             nc.scalar.activation(slot_bias[h][:], bias_rows[h][:].indirect(buckets[:]), ACT.Copy)
@@ -135,11 +148,11 @@ def tile_attend_mixedbias_pl_kernel(
         v_scales = sb.tile([P, E], U8, align_bytes=64)
         exps = [
             placed.tile([P, 2, PACK, P], F32, name="exps0", offset=EXP_AT),
-            sb.tile([P, 2, PACK, P], F32, name="exps1"),
+            placed.tile([P, 2, PACK, P], F32, name="exps1", offset=PLAIN_AT),
         ]
         sums = sb.tile([P, 2 * HALVES], F32)
         inv = sb.tile([P, 2 * HALVES], F32)
-        biased = [sb.tile([P, I], F32, name="biased%d" % h) for h in range(HALVES)]
+        biased = [placed.tile([P, I], F32, name="biased0", offset=NEG_AT), sb.tile([P, I], F32, name="biased1")]
         neg_max_a = [
             placed.tile([P, 1], F32, name="neg_max_a0", offset=Q_RAW_AT),
             sb.tile([P, 1], F32, name="neg_max_a1"),
@@ -214,7 +227,7 @@ def tile_attend_mixedbias_pl_kernel(
             )
 
         listed = [
-            sb.tile([P, I], BF16, name="listed0"),
+            placed.tile([P, I], BF16, name="listed0", offset=NEG_AT),
             placed.tile([P, I], BF16, name="listed1", offset=EXP_AT),
             sb.tile([P, I], BF16, name="listed2"),
             sb.tile([P, I], BF16, name="listed3"),

@@ -65,15 +65,16 @@ def tile_attend_mixedbias_pl_kernel(
         for h in range(HALVES):
             nc.gpsimd.memset(bias_rows[h][:, U:], 0.0)
         make_identity(nc, ident[:])
+        with nc.allow_non_contiguous_dma(reason="one gate for each partition and half"):
+            nc.gpsimd.dma_start(gates[:], gate.rearrange("(h p) o -> p h o", p=P))
+        nc.gpsimd.dma_start(sizes[:], size.rearrange("o (p t) -> p (o t)", t=PACK))
 
         q_dealt = query.rearrange("(p j) q -> p j q", j=PACK)
         nc.sync.dma_start(slots[:], offs)
-        nc.sync.dma_start(key_scales[SCALES_AT:, :].bitcast(I32), keys_scales[0].bitcast(I32))
+        nc.scalar.dma_start(key_scales[SCALES_AT:, :].bitcast(I32), keys_scales[0].bitcast(I32))
         nc.sync.dma_start(q_raw[0][:], q_dealt[:, :, :P])
         nc.sync.dma_start(key_words[:].bitcast(I32), keys_words[0].bitcast(I32))
         nc.sync.dma_start(buckets[:], offs2)
-        with nc.allow_non_contiguous_dma(reason="one gate for each partition and half"):
-            nc.sync.dma_start(gates[:], gate.rearrange("(h p) o -> p h o", p=P))
         nc.sync.dma_start(bias_rows[0][:, :U], bias[:P, :])
         nc.sync.dma_start(q_raw[1][:], q_dealt[:, :, P:])
         nc.sync.dma_start(bias_rows[1][:, :U], bias[P:, :])
@@ -85,7 +86,6 @@ def tile_attend_mixedbias_pl_kernel(
             )
         vals_dealt = vals.rearrange("(p r) t -> r p t", r=PACK)
         nc.sync.dma_start(v_raw[0][:], vals_dealt[0])
-        nc.sync.dma_start(sizes[:], size.rearrange("o (p t) -> p (o t)", t=PACK))
         for r in range(1, PACK):
             nc.sync.dma_start(v_raw[r][:], vals_dealt[r])
 

@@ -28,8 +28,8 @@ ROW_BYTES = 4 * T
 Q_RAW_AT = PACK * ROW_BYTES
 EXP_AT = Q_RAW_AT + 8 * I
 Q_BF_AT = EXP_AT + 8 * I
-PLAIN_AT = Q_BF_AT + 2 * I
-NEG_AT = PLAIN_AT + 8 * I
+PLAIN_AT = (EXP_AT, EXP_AT + 4 * I)
+FIRST_SPLIT = 20
 LAST_SPLIT = 16
 
 
@@ -85,8 +85,7 @@ def tile_attend_mixedbias_pl_kernel(
                 listed_scales[SCALES_AT + c : P : 4, :].bitcast(I32),
             )
         vals_dealt = vals.rearrange("(p r) t -> r p t", r=PACK)
-        nc.sync.dma_start(v_raw[0][:], vals_dealt[0])
-        for r in range(1, PACK):
+        for r in range(PACK):
             nc.sync.dma_start(v_raw[r][:], vals_dealt[r])
 
         slot_bias = [sb.tile([P, I], F32, name="slot_bias%d" % h) for h in range(HALVES)]
@@ -134,69 +133,55 @@ def tile_attend_mixedbias_pl_kernel(
         nc.gpsimd.tensor_scalar(rest[:], gates[:], -1.0, 1.0, ALU.mult, ALU.add)
         shares = (gates, rest)
 
-        last = (PACK - 1) * ROW_BYTES
-        w_bf = [None] * HALVES
-        w_codes = placed.tile([P, Q], U32, align_bytes=64, offset=last + 1024)
+        last = 3 * ROW_BYTES
         w_scales = sb.tile([P, Q], U8, align_bytes=64)
-        v_bf = [
-            placed.tile([P, I], BF16, align_bytes=64, name="v_bf0", offset=ROW_BYTES)[:],
-            placed.tile([P, I], BF16, align_bytes=64, name="v_bf1", offset=last + 2048)[:],
-            placed.tile([P, I], BF16, align_bytes=64, name="v_bf2", offset=last + 3072)[:],
-            sb.tile([P, I], BF16, align_bytes=64, name="v_bf3")[:],
-        ]
-        v_codes = placed.tile([P, E], U32, align_bytes=64, offset=last + 4096)
         v_scales = sb.tile([P, E], U8, align_bytes=64)
         exps = [
-            placed.tile([P, 2, PACK, P], F32, name="exps0", offset=EXP_AT),
-            placed.tile([P, 2, PACK, P], F32, name="exps1", offset=PLAIN_AT),
+            [
+                sb.tile([P, PACK, P], F32, name="biased_exps%d" % h),
+                placed.tile([P, PACK, P], F32, name="plain_exps%d" % h, offset=PLAIN_AT[h]),
+            ]
+            for h in range(HALVES)
         ]
         sums = sb.tile([P, 2 * HALVES], F32)
         inv = sb.tile([P, 2 * HALVES], F32)
-        biased = [placed.tile([P, I], F32, name="biased0", offset=NEG_AT), sb.tile([P, I], F32, name="biased1")]
-        neg_max_a = [
-            placed.tile([P, 1], F32, name="neg_max_a0", offset=Q_RAW_AT),
-            sb.tile([P, 1], F32, name="neg_max_a1"),
-        ]
-        neg_max_s = [sb.tile([P, 1], F32, name="neg_max_s%d" % h) for h in range(HALVES)]
+        biased = [sb.tile([P, I], F32, name="biased%d" % h) for h in range(HALVES)]
+        neg_max = [[sb.tile([P, 1], F32, name="neg_max%d%d" % (h, k)) for k in range(2)] for h in range(HALVES)]
         parts = [sb.tile([P, 2, PACK, P], F32, name="parts%d" % h) for h in range(HALVES)]
-        coef = [sb.tile([P, 2], F32, name="coef%d" % h) for h in range(HALVES)]
         w_turned = [ps.tile([P, PACK, P], F32, name="w_turned%d" % h, tag="w_turned%d" % h) for h in range(HALVES)]
 
         def plain_max(h):
-            nc.vector.tensor_reduce(neg_max_a[h][:], scores[h][:], AX.X, ALU.max, negate=True)
+            nc.vector.tensor_reduce(neg_max[h][1][:], scores[h][:], AX.X, ALU.max, negate=True)
+
+        def plain_exp(h):
+            nc.scalar.activation(
+                exps[h][1][:],
+                scores[h][:].rearrange("p (s t) -> p t s", t=PACK),
+                ACT.Exp,
+                bias=neg_max[h][1][:],
+                accum_out=sums[:, 2 * h + 1 : 2 * h + 2],
+            )
 
         def add_bias(h):
             nc.vector.tensor_tensor(biased[h][:], scores[h][:], slot_bias[h][:], ALU.add)
-            nc.scalar.activation(
-                exps[h][:, 1],
-                scores[h][:].rearrange("p (s t) -> p t s", t=PACK),
-                ACT.Exp,
-                bias=neg_max_a[h][:],
-                accum_out=sums[:, h : h + 1],
-            )
 
         def biased_exp(h):
-            nc.vector.tensor_reduce(neg_max_s[h][:], biased[h][:], AX.X, ALU.max, negate=True)
+            nc.vector.tensor_reduce(neg_max[h][0][:], biased[h][:], AX.X, ALU.max, negate=True)
             nc.scalar.activation(
-                exps[h][:, 0].rearrange("p t s -> p s t"),
+                exps[h][0][:].rearrange("p t s -> p s t"),
                 biased[h][:].rearrange("p (s t) -> p s t", t=PACK),
                 ACT.Exp,
-                bias=neg_max_s[h][:],
-                accum_out=sums[:, HALVES + h : HALVES + h + 1],
+                bias=neg_max[h][0][:],
+                accum_out=sums[:, 2 * h : 2 * h + 1],
             )
+
+        def invert(h, k):
+            at = slice(2 * h + k, 2 * h + k + 1)
+            nc.vector.reciprocal(inv[:, at], sums[:, at])
 
         def scale_part(h, k):
-            at = (1 - k) * HALVES + h
-            nc.scalar.activation(coef[h][:, k : k + 1], inv[:, at : at + 1], ACT.Copy, scale=shares[k][:, h, :])
-            nc.scalar.activation(parts[h][:, k], exps[h][:, k], ACT.Copy, scale=coef[h][:, k : k + 1])
-
-        def scale_on_vector(h, k):
-            at = (1 - k) * HALVES + h
-            nc.vector.tensor_scalar(
-                parts[h][:, k], exps[h][:, k], inv[:, at : at + 1], shares[k][:, h, :], ALU.mult, ALU.mult
-            )
-
-        def turn_part(h, k):
+            at = slice(2 * h + k, 2 * h + k + 1)
+            nc.vector.tensor_scalar(parts[h][:, k], exps[h][k][:], inv[:, at], shares[k][:, h, :], ALU.mult, ALU.mult)
             for t in range(PACK):
                 nc.tensor.matmul(
                     w_turned[h][:, t, :],
@@ -207,51 +192,43 @@ def tile_attend_mixedbias_pl_kernel(
                     is_transpose=True,
                 )
 
-        def round_weights(h):
-            w_bf[h] = placed.tile(
-                [P, P, PACK], BF16, align_bytes=64, name="w_bf%d" % h, offset=(2 + h) * ROW_BYTES
-            )
+        def round_weights(h, w_bf):
             nc.vector.tensor_tensor(
-                w_bf[h][:],
+                w_bf[:],
                 w_turned[h][:].rearrange("p t q -> p q t"),
                 sizes[:].unsqueeze(1).to_broadcast([P, P, PACK]),
                 ALU.mult,
             )
 
-        def quantise_weights(h):
+        def quantise_weights(h, w_bf):
             cols = slice(h * P, (h + 1) * P)
             nc.vector.quantize_mx(
                 out=w_codes[:, cols].bitcast(FP8X4),
                 scales=w_scales[:, cols],
-                in_=w_bf[h][:].rearrange("p q t -> p (q t)"),
+                in_=w_bf[:].rearrange("p q t -> p (q t)"),
             )
 
-        listed = [
-            placed.tile([P, I], BF16, name="listed0", offset=NEG_AT),
-            placed.tile([P, I], BF16, name="listed1", offset=EXP_AT),
-            sb.tile([P, I], BF16, name="listed2"),
-            sb.tile([P, I], BF16, name="listed3"),
-        ]
-
-        def gather_values(r):
-            nc.vector.tensor_copy(listed[r][:], v_raw[r][:].indirect(slots[:]))
-
-        def turn_values(r):
-            pairs = listed[r][:].bitcast(F32)
-            turned = ps.tile([P, 2, P], F32, name="turned%d" % r, tag=("turned0", "turned1", "bank2", "bank3")[r])
+        def gather_values(r, listed, split):
+            at = 16 * split
+            if split > 0:
+                nc.vector.tensor_copy(listed[:, :at], v_raw[r][:].indirect(slots[:, :split]))
+            if at < I:
+                nc.scalar.activation(listed[:, at:], v_raw[r][:].indirect(slots[:, split:]), ACT.Copy)
+            pairs = listed[:].bitcast(F32)
+            turned = ps.tile([P, 2, P], F32, name="turned%d" % r, tag="bank%d" % (r + 2))
             for u in range(2):
                 nc.tensor.transpose(turned[:, u, :], pairs[:, u::2], ident[:])
             return turned
 
-        def copy_values(r, turned):
-            nc.scalar.copy(
-                v_bf[r].bitcast(F32).rearrange("p (m u) -> p m u", u=2),
+        def copy_values(copy, v_bf, turned):
+            copy(
+                v_bf[:].bitcast(F32).rearrange("p (m u) -> p m u", u=2),
                 turned[:].rearrange("p u m -> p m u"),
             )
 
-        def quantise_values(first, rounded):
-            feats = slice(first * P, first * P + rounded.shape[1] // PACK)
-            nc.vector.quantize_mx(out=v_codes[:, feats].bitcast(FP8X4), scales=v_scales[:, feats], in_=rounded)
+        def quantise_values(r, v_bf):
+            feats = slice(r * P, (r + 1) * P)
+            nc.vector.quantize_mx(out=v_codes[:, feats].bitcast(FP8X4), scales=v_scales[:, feats], in_=v_bf[:])
 
         def product(out, r, h):
             cols = slice(h * P, (h + 1) * P)
@@ -266,43 +243,47 @@ def tile_attend_mixedbias_pl_kernel(
                 stop=True,
             )
 
+        v_codes = sb.tile([P, E], U32, align_bytes=64)
+        w_bf0 = sb.tile([P, P, PACK], BF16, align_bytes=64)
+        w_codes = sb.tile([P, Q], U32, align_bytes=64)
+        listed = [
+            placed.tile([P, I], BF16, name="listed0", offset=PLAIN_AT[0]),
+            placed.tile([P, I], BF16, name="listed1", offset=PLAIN_AT[1]),
+            sb.tile([P, I], BF16, name="listed2"),
+            sb.tile([P, I], BF16, name="listed3"),
+        ]
         for h in range(HALVES):
             plain_max(h)
             add_bias(h)
-        nc.vector.reciprocal(inv[:, 0:1], sums[:, 0:1])
+            plain_exp(h)
+        invert(0, 1)
         for h in range(HALVES):
             biased_exp(h)
-        nc.vector.reciprocal(inv[:, 1:2], sums[:, 1:2])
-        for h in range(HALVES):
-            scale_on_vector(h, 1)
-            turn_part(h, 1)
-        nc.vector.reciprocal(inv[:, 2:3], sums[:, 2:3])
+        invert(1, 1)
+        scale_part(0, 1)
+        invert(0, 0)
+        scale_part(1, 1)
         scale_part(0, 0)
-        turn_part(0, 0)
-        gather_values(0)
-        nc.vector.reciprocal(inv[:, 3:4], sums[:, 3:4])
-        scale_on_vector(1, 0)
-        turn_part(1, 0)
-        turned = [turn_values(0)]
-        nc.scalar.activation(listed[1][:], v_raw[1][:].indirect(slots[:]), ACT.Copy)
-        turned.append(turn_values(1))
-        gather_values(2)
-        turned.append(turn_values(2))
-        copy_values(0, turned[0])
-        round_weights(0)
-        shared = 16 * LAST_SPLIT
-        nc.vector.tensor_copy(listed[3][:, :shared], v_raw[3][:].indirect(slots[:, :LAST_SPLIT]))
-        nc.scalar.activation(listed[3][:, shared:], v_raw[3][:].indirect(slots[:, LAST_SPLIT:]), ACT.Copy)
-        turned.append(turn_values(3))
-        for r in range(1, PACK):
-            copy_values(r, turned[r])
-        quantise_weights(0)
+        invert(1, 0)
+        turned = [gather_values(0, listed[0], FIRST_SPLIT)]
+        scale_part(1, 0)
+        turned.append(gather_values(1, listed[1], 0))
+        round_weights(0, w_bf0)
+        quantise_weights(0, w_bf0)
+        turned.append(gather_values(2, listed[2], 0))
+        turned.append(gather_values(3, listed[3], LAST_SPLIT))
+        w_bf1 = placed.tile([P, P, PACK], BF16, align_bytes=64, offset=last)
+        v_bf = [
+            placed.tile([P, I], BF16, align_bytes=64, name="v_bf%d" % r, offset=last + (r + 1) * 1024)
+            for r in range(PACK)
+        ]
+        for r in range(PACK):
+            copy_values(nc.scalar.copy, v_bf[r], turned[r])
+        round_weights(1, w_bf1)
         quantise_values(0, v_bf[0])
-        round_weights(1)
-        quantise_values(1, v_bf[1])
-        quantise_values(2, v_bf[2])
-        quantise_weights(1)
-        quantise_values(3, v_bf[3])
+        quantise_weights(1, w_bf1)
+        for r in range(1, PACK):
+            quantise_values(r, v_bf[r])
 
         out_rows = out_0.rearrange("(p r) q -> p r q", r=PACK)
         o_f32 = [sb.tile([P, PACK, P], F32, align_bytes=256, name="o_f32_%d" % h) for h in range(HALVES)]

@@ -29,7 +29,7 @@ Q_RAW_AT = PACK * ROW_BYTES
 EXP_AT = Q_RAW_AT + 8 * I
 Q_BF_AT = EXP_AT + 8 * I
 PLAIN_AT = (EXP_AT, EXP_AT + 4 * I)
-FIRST_SPLIT = 20
+FIRST_SPLIT = 28
 LAST_SPLIT = 16
 
 
@@ -247,27 +247,29 @@ def tile_attend_mixedbias_pl_kernel(
         w_bf0 = sb.tile([P, P, PACK], BF16, align_bytes=64)
         w_codes = sb.tile([P, Q], U32, align_bytes=64)
         listed = [
-            placed.tile([P, I], BF16, name="listed0", offset=PLAIN_AT[0]),
-            placed.tile([P, I], BF16, name="listed1", offset=PLAIN_AT[1]),
+            placed.tile([P, I], BF16, name="listed0", offset=PLAIN_AT[1]),
+            placed.tile([P, I], BF16, name="listed1", offset=PLAIN_AT[0]),
             sb.tile([P, I], BF16, name="listed2"),
             sb.tile([P, I], BF16, name="listed3"),
         ]
-        for h in range(HALVES):
-            plain_max(h)
-            add_bias(h)
-            plain_exp(h)
+        plain_max(0)
+        add_bias(0)
+        plain_exp(0)
+        plain_max(1)
+        biased_exp(0)
         invert(0, 1)
-        for h in range(HALVES):
-            biased_exp(h)
-        invert(1, 1)
+        add_bias(1)
+        plain_exp(1)
         scale_part(0, 1)
+        biased_exp(1)
         invert(0, 0)
-        scale_part(1, 1)
+        invert(1, 1)
         scale_part(0, 0)
+        scale_part(1, 1)
         invert(1, 0)
-        turned = [gather_values(0, listed[0], FIRST_SPLIT)]
+        second = gather_values(1, listed[1], 0)
+        turned = [gather_values(0, listed[0], FIRST_SPLIT), second]
         scale_part(1, 0)
-        turned.append(gather_values(1, listed[1], 0))
         round_weights(0, w_bf0)
         quantise_weights(0, w_bf0)
         turned.append(gather_values(2, listed[2], 0))

@@ -61,17 +61,18 @@ def tile_attend_mixedbias_pl_kernel(
         gates = sb.tile([P, HALVES, 1], F32)
         sizes = sb.tile([P, PACK], F32)
         nc.vector.memset(key_scales[:SCALES_AT, :].bitcast(I32), 0)
+        gate_rows = sb.tile([P, P], F32, align_bytes=256)
+        nc.gpsimd.memset(gate_rows[: P - HALVES, :], 0.0)
         nc.gpsimd.memset(k_scales[:].bitcast(I32), 0)
         for h in range(HALVES):
             nc.gpsimd.memset(bias_rows[h][:, U:], 0.0)
         make_identity(nc, ident[:])
-        with nc.allow_non_contiguous_dma(reason="one gate for each partition and half"):
-            nc.gpsimd.dma_start(gates[:], gate.rearrange("(h p) o -> p h o", p=P))
         nc.gpsimd.dma_start(sizes[:], size.rearrange("o (p t) -> p (o t)", t=PACK))
 
         q_dealt = query.rearrange("(p j) q -> p j q", j=PACK)
         nc.sync.dma_start(slots[:], offs)
         nc.scalar.dma_start(key_scales[SCALES_AT:, :].bitcast(I32), keys_scales[0].bitcast(I32))
+        nc.scalar.dma_start(gate_rows[P - HALVES :, :], gate.rearrange("(h p) o -> h (p o)", p=P))
         nc.sync.dma_start(q_raw[0][:], q_dealt[:, :, :P])
         nc.sync.dma_start(key_words[:].bitcast(I32), keys_words[0].bitcast(I32))
         nc.sync.dma_start(buckets[:], offs2)
@@ -98,6 +99,9 @@ def tile_attend_mixedbias_pl_kernel(
         scores = [ps.tile([P, I], F32, name="scores%d" % h, tag="bank%d" % h) for h in range(HALVES)]
 
         nc.scalar.copy(q_bf[0][:], q_raw[0][:].rearrange("p j q -> p q j"))
+        gates_turned = ps.tile([P, P], F32, tag="bank5")
+        nc.tensor.transpose(gates_turned[:], gate_rows[:], ident[:])
+        nc.scalar.copy(gates[:, :, 0], gates_turned[:, P - HALVES :])
 
         def quantise_queries(h):
             cols = slice(h * P, (h + 1) * P)

@@ -292,12 +292,13 @@ def tile_attend_mixedbias_pl_kernel(
             quantise_values(r, v_bf[r])
 
         out_rows = out_0.rearrange("(p r) q -> p r q", r=PACK)
-        o_f32 = [sb.tile([P, PACK, P], F32, align_bytes=256, name="o_f32_%d" % h) for h in range(HALVES)]
+        o_rows = sb.tile([P, PACK, Q], F32, align_bytes=256)
+        o_f32 = [o_rows[:, :, h * P : (h + 1) * P] for h in range(HALVES)]
         o_bf = [sb.tile([P, P, PACK], BF16, align_bytes=64, name="o_bf%d" % h) for h in range(HALVES)]
         o_codes = sb.tile([P, Q], U32, align_bytes=256)
         o_scales = sb.tile([P, Q], U8, align_bytes=256)
-        groups = (((0, 1), (2,), (3,)), ((0, 1), (2, 3)))
-        banks = (("bank0", "bank1", "w_turned0"), ("bank2", "bank3"))
+        groups = (((0, 1), (2,), (3,)),) * HALVES
+        banks = (("bank0", "bank1", "w_turned0"), ("bank2", "bank3", "w_turned1"))
         results = {}
         for h in range(HALVES):
             for rows, bank in zip(groups[h], banks[h]):
@@ -309,13 +310,14 @@ def tile_attend_mixedbias_pl_kernel(
                 held, rows = results[h, r]
                 product(held[:, r - rows[0], :], r, h)
                 if r == rows[-1]:
-                    nc.scalar.copy(o_f32[h][:, rows[0] : r + 1, :], held[:])
+                    copy = nc.vector.tensor_copy if (h, r) == (1, 1) else nc.scalar.copy
+                    copy(o_f32[h][:, rows[0] : r + 1, :], held[:])
+        nc.sync.dma_start(out_rows[:, : PACK - 1, :], o_rows[:, : PACK - 1, :])
+        nc.sync.dma_start(out_rows[:, PACK - 1, :], o_rows[:, PACK - 1, :])
         for h in range(HALVES):
-            cols = slice(h * P, (h + 1) * P)
-            nc.sync.dma_start(out_rows[:, :, cols], o_f32[h][:])
             nc.vector.tensor_copy(
                 o_bf[h][:].rearrange("p (c i) r -> p c r i", i=4),
-                o_f32[h][:].rearrange("p r (c i) -> p c r i", i=4),
+                o_f32[h].rearrange("p r (c i) -> p c r i", i=4),
             )
         for h in range(HALVES):
             cols = slice(h * P, (h + 1) * P)

@@ -74,9 +74,9 @@ def tile_attend_mixedbias_pl_kernel(
         nc.scalar.dma_start(key_scales[SCALES_AT:, :].bitcast(I32), keys_scales[0].bitcast(I32))
         nc.scalar.dma_start(gate_rows[P - HALVES :, :], gate.rearrange("(h p) o -> h (p o)", p=P))
         nc.sync.dma_start(q_raw[0][:], q_dealt[:, :, :P])
-        nc.sync.dma_start(key_words[:].bitcast(I32), keys_words[0].bitcast(I32))
         nc.sync.dma_start(buckets[:], offs2)
         nc.sync.dma_start(bias_rows[0][:, :U], bias[:P, :])
+        nc.sync.dma_start(key_words[:].bitcast(I32), keys_words[0].bitcast(I32))
         nc.sync.dma_start(q_raw[1][:], q_dealt[:, :, P:])
         nc.sync.dma_start(bias_rows[1][:, :U], bias[P:, :])
         nc.vector.tensor_copy(listed_scales[:], key_scales[:].indirect(slots[:]))

from contextlib import ExitStack

import concourse.mybir as mybir
from concourse.masks import make_identity

D, T, I, Q, E, U = 512, 2048, 512, 256, 512, 512
FLOPS = 2 * D * Q * I + 2 * I * E * Q

F32 = mybir.dt.float32
BF16 = mybir.dt.bfloat16
I32 = mybir.dt.int32
U32 = mybir.dt.uint32
U16 = mybir.dt.uint16
U8 = mybir.dt.uint8
FP8X4 = mybir.dt.float8_e4m3fn_x4
FP4X4 = mybir.dt.float4_e2m1fn_x4
ALU = mybir.AluOpType
ACT = mybir.ActivationFunctionType
AX = mybir.AxisListType

P = 128
PACK = 4
HALVES = Q // P
BIAS_WINDOW = U + 8
SCALE_ROWS = 16
SCALES_AT = P - SCALE_ROWS
ROW_BYTES = 4 * T
Q_RAW_AT = PACK * ROW_BYTES
EXP_AT = Q_RAW_AT + 8 * I
Q_BF_AT = EXP_AT + 8 * I
PLAIN_AT = (EXP_AT, EXP_AT + 4 * I)
FIRST_SPLIT = 28
LAST_SPLIT = 16


def tile_attend_mixedbias_pl_kernel(
    tc, query, keys_words, keys_scales, bias, gate, size, vals, offs, offs2, out_0, out_1, out_2
):
    nc = tc.nc
    with ExitStack() as ctx:
        sb = ctx.enter_context(tc.tile_pool(name="sb", bufs=1))
        placed = ctx.enter_context(tc.tile_pool(name="placed", bufs=1))
        ps = ctx.enter_context(tc.psum_pool(name="ps", bufs=1))

        slots = sb.tile([P, I // 16], U16)
        buckets = sb.tile([P, I // 16], U16)
        key_words = sb.tile([P, T], U16, align_bytes=256)
        key_scales = sb.tile([P, T], U8, align_bytes=256)
        q_raw = [
            placed.tile([P, PACK, P], F32, align_bytes=256, name="q_raw0", offset=Q_RAW_AT + 4 * I),
            placed.tile([P, PACK, P], F32, align_bytes=256, name="q_raw1", offset=Q_RAW_AT),
        ]
        bias_rows = [sb.tile([P, BIAS_WINDOW], F32, align_bytes=256, name="bias_rows%d" % h) for h in range(HALVES)]
        v_raw = [
            placed.tile([P, T], F32, align_bytes=256, name="v_raw%d" % r, offset=r * ROW_BYTES) for r in range(PACK)
        ]
        ident = sb.tile([P, P], F32)

        listed_scales = sb.tile([P, I], U8, align_bytes=256)
        k_scales = sb.tile([P, I], U8, align_bytes=256)
        gates = sb.tile([P, HALVES, 1], F32)
        sizes = sb.tile([P, PACK], F32)
        nc.vector.memset(key_scales[:SCALES_AT, :].bitcast(I32), 0)
        gate_rows = sb.tile([P, P], F32, align_bytes=256)
        nc.gpsimd.memset(gate_rows[: P - HALVES, :], 0.0)
        nc.gpsimd.memset(k_scales[:].bitcast(I32), 0)
        for h in range(HALVES):
            nc.gpsimd.memset(bias_rows[h][:, U:], 0.0)
        make_identity(nc, ident[:])
        nc.gpsimd.dma_start(sizes[:], size.rearrange("o (p t) -> p (o t)", t=PACK))

        q_dealt = query.rearrange("(p j) q -> p j q", j=PACK)
        nc.sync.dma_start(slots[:], offs)
        nc.scalar.dma_start(key_scales[SCALES_AT:, :].bitcast(I32), keys_scales[0].bitcast(I32))
        nc.scalar.dma_start(gate_rows[P - HALVES :, :], gate.rearrange("(h p) o -> h (p o)", p=P))
        nc.sync.dma_start(q_raw[0][:], q_dealt[:, :, :P])
        nc.sync.dma_start(buckets[:], offs2)
        nc.sync.dma_start(bias_rows[0][:, :U], bias[:P, :])
        nc.sync.dma_start(key_words[:].bitcast(I32), keys_words[0].bitcast(I32))
        nc.sync.dma_start(q_raw[1][:], q_dealt[:, :, P:])
        nc.sync.dma_start(bias_rows[1][:, :U], bias[P:, :])
        nc.vector.tensor_copy(listed_scales[:], key_scales[:].indirect(slots[:]))
        for c in range(4):
            nc.sync.dma_start(
                k_scales[c:P:32, :].bitcast(I32),
                listed_scales[SCALES_AT + c : P : 4, :].bitcast(I32),
            )
        vals_dealt = vals.rearrange("(p r) t -> r p t", r=PACK)
        for r in range(PACK):
            nc.sync.dma_start(v_raw[r][:], vals_dealt[r])

        slot_bias = [sb.tile([P, I], F32, name="slot_bias%d" % h) for h in range(HALVES)]
        q_bf = [
            placed.tile([P, P, PACK], BF16, align_bytes=64, name="q_bf0", offset=Q_BF_AT),
            sb.tile([P, P, PACK], BF16, align_bytes=64, name="q_bf1"),
        ]
        q_codes = sb.tile([P, Q], U32, align_bytes=64)
        q_scales = sb.tile([P, Q], U8, align_bytes=64)
        scores = [ps.tile([P, I], F32, name="scores%d" % h, tag="bank%d" % h) for h in range(HALVES)]

        nc.scalar.copy(q_bf[0][:], q_raw[0][:].rearrange("p j q -> p q j"))
        gates_turned = ps.tile([P, P], F32, tag="bank5")
        nc.tensor.transpose(gates_turned[:], gate_rows[:], ident[:])
        nc.scalar.copy(gates[:, :, 0], gates_turned[:, P - HALVES :])

        def quantise_queries(h):
            cols = slice(h * P, (h + 1) * P)
            nc.vector.quantize_mx(
                out=q_codes[:, cols].bitcast(FP8X4),
                scales=q_scales[:, cols],
                in_=q_bf[h][:].rearrange("p q j -> p (q j)"),
            )

        def score(h):
            cols = slice(h * P, (h + 1) * P)
            nc.tensor.matmul_mx(
                out=scores[h][:],
                lhsT=q_codes[:, cols].bitcast(FP8X4),
                lhsT_scale=q_scales[:, cols],
                rhs=k_words[:].bitcast(FP4X4),
                rhs_scale=k_scales[:],
                start=True,
                stop=True,
            )

        quantise_queries(0)
        k_words = placed.tile([P, I], U16, align_bytes=64, offset=Q_BF_AT)
        nc.vector.tensor_copy(k_words[:], key_words[:].indirect(slots[:]))
        score(0)
        nc.vector.tensor_copy(q_bf[1][:], q_raw[1][:].rearrange("p j q -> p q j"))
        quantise_queries(1)
        score(1)
        for h in range(HALVES):
            nc.scalar.activation(slot_bias[h][:], bias_rows[h][:].indirect(buckets[:]), ACT.Copy)

        rest = sb.tile([P, HALVES, 1], F32)
        nc.gpsimd.tensor_scalar(rest[:], gates[:], -1.0, 1.0, ALU.mult, ALU.add)
        shares = (gates, rest)

        last = 3 * ROW_BYTES
        w_scales = sb.tile([P, Q], U8, align_bytes=64)
        v_scales = sb.tile([P, E], U8, align_bytes=64)
        exps = [
            [
                sb.tile([P, PACK, P], F32, name="biased_exps%d" % h),
                placed.tile([P, PACK, P], F32, name="plain_exps%d" % h, offset=PLAIN_AT[h]),
            ]
            for h in range(HALVES)
        ]
        sums = sb.tile([P, 2 * HALVES], F32)
        inv = sb.tile([P, 2 * HALVES], F32)
        biased = [sb.tile([P, I], F32, name="biased%d" % h) for h in range(HALVES)]
        neg_max = [[sb.tile([P, 1], F32, name="neg_max%d%d" % (h, k)) for k in range(2)] for h in range(HALVES)]
        parts = [sb.tile([P, 2, PACK, P], F32, name="parts%d" % h) for h in range(HALVES)]
        w_turned = [ps.tile([P, PACK, P], F32, name="w_turned%d" % h, tag="w_turned%d" % h) for h in range(HALVES)]

        def plain_max(h):
            nc.vector.tensor_reduce(neg_max[h][1][:], scores[h][:], AX.X, ALU.max, negate=True)

        def plain_exp(h):
            nc.scalar.activation(
                exps[h][1][:],
                scores[h][:].rearrange("p (s t) -> p t s", t=PACK),
                ACT.Exp,
                bias=neg_max[h][1][:],
                accum_out=sums[:, 2 * h + 1 : 2 * h + 2],
            )

        def add_bias(h):
            nc.vector.tensor_tensor(biased[h][:], scores[h][:], slot_bias[h][:], ALU.add)

        def biased_exp(h):
            nc.vector.tensor_reduce(neg_max[h][0][:], biased[h][:], AX.X, ALU.max, negate=True)
            nc.scalar.activation(
                exps[h][0][:].rearrange("p t s -> p s t"),
                biased[h][:].rearrange("p (s t) -> p s t", t=PACK),
                ACT.Exp,
                bias=neg_max[h][0][:],
                accum_out=sums[:, 2 * h : 2 * h + 1],
            )

        def invert(h, k):
            at = slice(2 * h + k, 2 * h + k + 1)
            nc.vector.reciprocal(inv[:, at], sums[:, at])

        def scale_part(h, k):
            at = slice(2 * h + k, 2 * h + k + 1)
            nc.vector.tensor_scalar(parts[h][:, k], exps[h][k][:], inv[:, at], shares[k][:, h, :], ALU.mult, ALU.mult)
            for t in range(PACK):
                nc.tensor.matmul(
                    w_turned[h][:, t, :],
                    parts[h][:, k, t, :],
                    ident[:],
                    start=(k == 1 and t == 0),
                    stop=(k == 0 and t == PACK - 1),
                    is_transpose=True,
                )

        def round_weights(h, w_bf):
            nc.vector.tensor_tensor(
                w_bf[:],
                w_turned[h][:].rearrange("p t q -> p q t"),
                sizes[:].unsqueeze(1).to_broadcast([P, P, PACK]),
                ALU.mult,
            )

        def quantise_weights(h, w_bf):
            cols = slice(h * P, (h + 1) * P)
            nc.vector.quantize_mx(
                out=w_codes[:, cols].bitcast(FP8X4),
                scales=w_scales[:, cols],
                in_=w_bf[:].rearrange("p q t -> p (q t)"),
            )

        def gather_values(r, listed, split):
            at = 16 * split
            if split > 0:
                nc.vector.tensor_copy(listed[:, :at], v_raw[r][:].indirect(slots[:, :split]))
            if at < I:
                nc.scalar.activation(listed[:, at:], v_raw[r][:].indirect(slots[:, split:]), ACT.Copy)
            pairs = listed[:].bitcast(F32)
            turned = ps.tile([P, 2, P], F32, name="turned%d" % r, tag="bank%d" % (r + 2))
            for u in range(2):
                nc.tensor.transpose(turned[:, u, :], pairs[:, u::2], ident[:])
            return turned

        def copy_values(copy, v_bf, turned):
            copy(
                v_bf[:].bitcast(F32).rearrange("p (m u) -> p m u", u=2),
                turned[:].rearrange("p u m -> p m u"),
            )

        def quantise_values(r, v_bf):
            feats = slice(r * P, (r + 1) * P)
            nc.vector.quantize_mx(out=v_codes[:, feats].bitcast(FP8X4), scales=v_scales[:, feats], in_=v_bf[:])

        def product(out, r, h):
            cols = slice(h * P, (h + 1) * P)
            feats = slice(r * P, (r + 1) * P)
            nc.tensor.matmul_mx(
                out=out,
                lhsT=v_codes[:, feats].bitcast(FP8X4),
                lhsT_scale=v_scales[:, feats],
                rhs=w_codes[:, cols].bitcast(FP8X4),
                rhs_scale=w_scales[:, cols],
                start=True,
                stop=True,
            )

        v_codes = sb.tile([P, E], U32, align_bytes=64)
        w_bf0 = sb.tile([P, P, PACK], BF16, align_bytes=64)
        w_codes = sb.tile([P, Q], U32, align_bytes=64)
        listed = [
            placed.tile([P, I], BF16, name="listed0", offset=PLAIN_AT[1]),
            placed.tile([P, I], BF16, name="listed1", offset=PLAIN_AT[0]),
            sb.tile([P, I], BF16, name="listed2"),
            sb.tile([P, I], BF16, name="listed3"),
        ]
        plain_max(0)
        add_bias(0)
        plain_exp(0)
        plain_max(1)
        biased_exp(0)
        invert(0, 1)
        add_bias(1)
        plain_exp(1)
        scale_part(0, 1)
        biased_exp(1)
        invert(0, 0)
        invert(1, 1)
        scale_part(0, 0)
        scale_part(1, 1)
        invert(1, 0)
        second = gather_values(1, listed[1], 0)
        turned = [gather_values(0, listed[0], FIRST_SPLIT), second]
        scale_part(1, 0)
        round_weights(0, w_bf0)
        quantise_weights(0, w_bf0)
        turned.append(gather_values(2, listed[2], 0))
        turned.append(gather_values(3, listed[3], LAST_SPLIT))
        w_bf1 = placed.tile([P, P, PACK], BF16, align_bytes=64, offset=last)
        v_bf = [
            placed.tile([P, I], BF16, align_bytes=64, name="v_bf%d" % r, offset=last + (r + 1) * 1024)
            for r in range(PACK)
        ]
        for r in range(PACK):
            copy_values(nc.scalar.copy, v_bf[r], turned[r])
        round_weights(1, w_bf1)
        quantise_values(0, v_bf[0])
        quantise_weights(1, w_bf1)
        for r in range(1, PACK):
            quantise_values(r, v_bf[r])

        out_rows = out_0.rearrange("(p r) q -> p r q", r=PACK)
        o_rows = sb.tile([P, PACK, Q], F32, align_bytes=256)
        o_f32 = [o_rows[:, :, h * P : (h + 1) * P] for h in range(HALVES)]
        o_bf = [sb.tile([P, P, PACK], BF16, align_bytes=64, name="o_bf%d" % h) for h in range(HALVES)]
        o_codes = sb.tile([P, Q], U32, align_bytes=256)
        o_scales = sb.tile([P, Q], U8, align_bytes=256)
        groups = (((0, 1), (2,), (3,)),) * HALVES
        banks = (("bank0", "bank1", "w_turned0"), ("bank2", "bank3", "w_turned1"))
        results = {}
        for h in range(HALVES):
            for rows, bank in zip(groups[h], banks[h]):
                held = ps.tile([P, len(rows), P], F32, name="result%d%d" % (h, rows[0]), tag=bank)
                for r in rows:
                    results[h, r] = (held, rows)
        for r in range(PACK):
            for h in range(HALVES):
                held, rows = results[h, r]
                product(held[:, r - rows[0], :], r, h)
                if r == rows[-1]:
                    copy = nc.vector.tensor_copy if (h, r) == (1, 1) else nc.scalar.copy
                    copy(o_f32[h][:, rows[0] : r + 1, :], held[:])
        nc.sync.dma_start(out_rows[:, : PACK - 1, :], o_rows[:, : PACK - 1, :])
        nc.sync.dma_start(out_rows[:, PACK - 1, :], o_rows[:, PACK - 1, :])
        for h in range(HALVES):
            nc.vector.tensor_copy(
                o_bf[h][:].rearrange("p (c i) r -> p c r i", i=4),
                o_f32[h].rearrange("p r (c i) -> p c r i", i=4),
            )
        for h in range(HALVES):
            cols = slice(h * P, (h + 1) * P)
            nc.vector.quantize_mx(
                out=o_codes[:, cols].bitcast(FP8X4),
                scales=o_scales[:, cols],
                in_=o_bf[h][:].rearrange("p q r -> p (q r)"),
            )
        nc.sync.dma_start(out_1[0].rearrange("p q r -> p (q r)").bitcast(I32), o_codes[:].bitcast(I32))
        for c in range(4):
            queue = nc.sync if c < 2 else nc.scalar
            queue.dma_start(
                out_2[0, c:16:4, :].bitcast(I32),
                o_scales[c:P:32, :].bitcast(I32),
            )
